import numpy as np
import ml_dtypes


def mxq(x, axis, fmt="e4m3"):
    dtype, down = {"e4m3": (ml_dtypes.float8_e4m3fn, 7), "e5m2": (ml_dtypes.float8_e5m2, 14)}[fmt]
    v = np.moveaxis(np.asarray(x, np.float32).astype(ml_dtypes.bfloat16).astype(np.float64), axis, -1)
    blocks = v.reshape(v.shape[:-1] + (-1, 32))
    amax = np.abs(blocks).max(-1, keepdims=True)
    byte = np.maximum(np.where(amax > 0, np.frexp(amax)[1] - 1 + 127, 0) - down, 1)
    scale = np.exp2(byte - 127.0)
    codes = (blocks / scale).astype(np.float32).astype(dtype).astype(np.float64)
    return np.moveaxis((codes * scale).reshape(v.shape), -1, axis)


WIDE = False


def mx_kscale(k):
    if not WIDE:
        return np.ones(k)
    levels = np.array([10, -10, 5, -5, 0])
    if k % 512:
        return np.exp2(np.random.permutation(np.resize(levels, k // 32))).repeat(32)
    a = np.empty((k // 512, 16))
    for p in range(k // 512):
        a[p, :8] = np.random.permutation(np.resize(levels, 8))
        for g in range(8):
            far = levels[np.abs(levels - a[p, g]) >= 10]
            a[p, g + 8] = far[np.random.randint(len(far))]
    return np.exp2(a.ravel()).repeat(32)


def f64(x):
    return np.asarray(x).astype(np.float64)


def striped(idx):
    return np.tile(idx.reshape(-1, 16).T, (8, 1)).astype(np.uint16)


def unstriped(offs):
    return offs[:16].T.reshape(-1).astype(np.int64)


E2M1 = np.array([0.0, 0.5, 1.0, 1.5, 2.0, 3.0, 4.0, 6.0, -0.0, -0.5, -1.0, -1.5, -2.0, -3.0, -4.0, -6.0])


def pack_weight(w, fmt):
    k, n = w.shape
    w = f64(np.asarray(w, np.float32).astype(ml_dtypes.bfloat16)).reshape(k // 32, 32, n)
    amax = np.abs(w).max(1)
    if fmt == "e4m3":
        byte = np.frexp(amax)[1] - 1 + 127 - 7
    else:
        mant, ex = np.frexp(amax / 6.0)
        byte = np.where(mant > 0.5, ex, ex - 1) + 127
    byte = np.clip(np.where(amax > 0, byte, 1), 1, 254)
    scaled = (w * np.exp2(127.0 - byte)[:, None, :]).reshape(k, n).astype(np.float32)
    by_word = np.ascontiguousarray(scaled.reshape(k // 512, 128, 4, n).transpose(0, 1, 3, 2))
    if fmt == "e4m3":
        words = by_word.astype(ml_dtypes.float8_e4m3fn).view(np.uint8)
    else:
        c = by_word.astype(ml_dtypes.float4_e2m1fn).view(np.uint8) & 0xF
        words = (c[..., 0::2] | (c[..., 1::2] << 4)).reshape(k // 512, 128, 2 * n)
    return np.ascontiguousarray(words), np.ascontiguousarray(byte.astype(np.uint8).reshape(k // 512, 16, n))


def unpack_weight(words, scales, fmt):
    g, _, n = scales.shape
    words = np.ascontiguousarray(words).reshape(g, 128, n, -1)
    if fmt == "e4m3":
        vals = words.view(ml_dtypes.float8_e4m3fn).astype(np.float64)
    else:
        nib = np.empty((g, 128, n, 4), np.uint8)
        nib[..., 0::2] = words & 0xF
        nib[..., 1::2] = words >> 4
        vals = E2M1[nib]
    vals = vals * np.repeat(np.exp2(scales.astype(np.float64) - 127.0), 8, axis=1)[..., None]
    return vals.transpose(0, 1, 3, 2).reshape(g * 512, n)


def gelu(v):
    return 0.5 * v * (1.0 + np.tanh(np.sqrt(2.0 / np.pi) * (v + 0.044715 * v**3)))


K, H, T, S, P = 1536, 1024, 4096, 1024, 512


def setup_inputs():
    n = np.random.standard_normal
    s = mx_kscale(K)[:, None]
    u = mx_kscale(H)[:, None]
    tab_words, tab_scales = pack_weight(n((K, T)) * s, "e4m3")
    w1 = (1.5 * n((K, H)) / np.sqrt(K) / s).astype(np.float32)
    gain = (np.exp(0.3 * n(H)) * u[:, 0]).astype(np.float32)
    w2_words, w2_scales = pack_weight(1.2 * n((H, H)) / np.sqrt(H) / u, "e2m1")
    skip = np.random.uniform(0.4, 1.2, H).astype(np.float32)
    offs = striped(np.random.permutation(T)[:S])
    pos1 = striped(np.random.permutation(S)[:P])
    pos2 = striped(np.random.permutation(S)[:P])
    return {"tab_words": tab_words, "tab_scales": tab_scales, "offs": offs,
            "w1": w1, "pos1": pos1, "gain": gain,
            "w2_words": w2_words, "w2_scales": w2_scales,
            "pos2": pos2, "skip": skip}


def reference(tab_words, tab_scales, offs, w1, pos1, gain, w2_words, w2_scales, pos2, skip):
    v = unpack_weight(tab_words, tab_scales, "e4m3")[:, unstriped(offs)]
    h = mxq(f64(w1), 0, "e4m3").T @ v
    a = h[:, unstriped(pos1)]
    x = a / (1.0 + np.exp(-a)) * f64(gain)[:, None]
    w2 = unpack_weight(w2_words, w2_scales, "e2m1")
    y = w2.T @ mxq(x, 0, "e4m3")
    d = h[:, unstriped(pos2)]
    return y + f64(skip)[:, None] * d

@@ -1,0 +1,251 @@
+from contextlib import ExitStack
+
+import concourse.mybir as mybir
+
+K, H, T, S, M_OUT = 1536, 1024, 4096, 1024, 512
+FLOPS = 2 * K * H * S + 2 * H * H * M_OUT
+
+F32 = mybir.dt.float32
+BF16 = mybir.dt.bfloat16
+I32 = mybir.dt.int32
+U32 = mybir.dt.uint32
+U16 = mybir.dt.uint16
+U8 = mybir.dt.uint8
+FP8X4 = mybir.dt.float8_e4m3fn_x4
+FP4X4 = mybir.dt.float4_e2m1fn_x4
+SILU = mybir.ActivationFunctionType.Silu
+COPY = mybir.ActivationFunctionType.Copy
+MULT = mybir.AluOpType.mult
+ADD = mybir.AluOpType.add
+
+P = 128
+PACK = 4
+K_PASS = P * PACK
+BANK = 512
+K_PASSES = K // K_PASS
+BLOCKS = H // K_PASS
+
+
+def tile_list_ringing_residual_layer_kernel(
+    tc, tab_words, tab_scales, offs, w1, pos1, gain, w2_words, w2_scales, pos2, skip, out
+):
+    nc = tc.nc
+    with ExitStack() as ctx:
+        lists = ctx.enter_context(tc.tile_pool(name="lists", bufs=1))
+        sb = ctx.enter_context(tc.tile_pool(name="sb", bufs=1))
+        psum = ctx.enter_context(tc.psum_pool(name="psum", bufs=1))
+
+        def new_tile(shape, dtype, name, tag=None):
+            return sb.tile(shape, dtype, name=name, tag=tag or name, align_bytes=64)
+
+        offs_sb = lists.tile([P, S // 16], U16, name="offs_sb")
+        pos1_sb = lists.tile([P, M_OUT // 16], U16, name="pos1_sb")
+        pos2_sb = lists.tile([P, M_OUT // 16], U16, name="pos2_sb")
+
+        tab_planes = new_tile([P, T], U8, "tab_planes")
+        nc.vector.memset(tab_planes[:, 0 : T // 2].bitcast(I32), 0)
+        nc.gpsimd.memset(tab_planes[:, T // 2 : T].bitcast(I32), 0)
+        zero = new_tile([P, 1], F32, "zero")
+        nc.vector.memset(zero[:], 0.0)
+        silu_bias = new_tile([P, 1], F32, "silu_bias")
+        nc.scalar.activation(silu_bias[:], zero[:], SILU)
+        w2_planes = new_tile([P, BLOCKS * H], U8, "w2_planes")
+        nc.vector.memset(w2_planes[:].bitcast(I32), 0)
+
+        tab = [new_tile([P, T], I32, f"tab{a}") for a in range(K_PASSES)]
+
+        def load_tab(a):
+            nc.sync.dma_start(tab[a][:], tab_words[a].rearrange("p t i -> p (t i)").bitcast(I32))
+
+        def load_w1(a, c0, width, name, tag):
+            raw = new_tile([P, PACK, width], F32, name, tag)
+            rows = w1[a * K_PASS : (a + 1) * K_PASS, c0 : c0 + width]
+            nc.sync.dma_start(raw[:], rows.rearrange("(p j) c -> p j c", j=PACK))
+            return raw
+
+        nc.sync.dma_start(offs_sb[:], offs)
+        load_tab(0)
+        for q in range(4):
+            nc.sync.dma_start(
+                tab_planes[32 * q : 32 * q + 4 * K_PASSES, :].bitcast(I32),
+                tab_scales[:, 4 * q : 4 * q + 4, :].bitcast(I32),
+            )
+        raw = {}
+        raw[0, 0] = load_w1(0, 0, K_PASS, "raw00", "rawA")
+        load_tab(1)
+        raw[1, 0] = load_w1(1, 0, K_PASS, "raw10", "rawB")
+        for q in range(4):
+            nc.sync.dma_start(
+                w2_planes[32 * q : 32 * q + 4, :].bitcast(I32).rearrange("r (a c) -> r a c", a=BLOCKS),
+                w2_scales[:, 4 * q : 4 * q + 4, :].bitcast(I32).rearrange("a r c -> r a c"),
+            )
+        load_tab(2)
+        raw20 = [load_w1(2, u * 256, 256, f"raw20_{u}", f"raw20_{u}") for u in range(2)]
+        nc.sync.dma_start(pos1_sb[:], pos1)
+        nc.sync.dma_start(pos2_sb[:], pos2)
+
+        picked = [new_tile([P, S], U32, f"picked{a}") for a in range(K_PASSES)]
+        picked_planes = new_tile([P, S], U8, "picked_planes")
+
+        def pick_words(a):
+            nc.vector.tensor_copy(picked[a][:], tab[a][:].bitcast(U32).indirect(offs_sb[:]))
+
+        def interleave_w1(copy, grouped, src, m0, count):
+            copy(
+                grouped[:, :, m0 : m0 + count, :].rearrange("p t m j -> p m j t"),
+                src.rearrange("p j (m t) -> p m j t", t=PACK),
+            )
+
+        w1_codes = {}
+        w1_planes = {}
+
+        def quantise_w1(a, b, grouped, parts):
+            w1_codes[a, b] = new_tile([P, K_PASS], U32, f"w1_codes{a}{b}")
+            w1_planes[a, b] = new_tile([P, K_PASS], U8, f"w1_planes{a}{b}")
+            flat = grouped[:].rearrange("p t m j -> p (t m j)")
+            width = K_PASS // parts
+            for i in range(parts):
+                cols = slice(i * width, (i + 1) * width)
+                nc.vector.quantize_mx(
+                    out=w1_codes[a, b][:, cols].bitcast(FP8X4),
+                    scales=w1_planes[a, b][:, cols],
+                    in_=flat[:, PACK * i * width : PACK * (i + 1) * width],
+                )
+
+        banks = {}
+
+        def first_product(a, b, t):
+            for u in range(2):
+                if a == 0:
+                    banks[b, t, u] = psum.tile([P, BANK], F32, name=f"h_bank{b}{t}{u}", tag=f"bank{2 * t + u}")
+                rows = slice(t * P, (t + 1) * P)
+                cols = slice(u * BANK, (u + 1) * BANK)
+                nc.tensor.matmul_mx(
+                    out=banks[b, t, u][:],
+                    lhsT=w1_codes[a, b][:, rows].bitcast(FP8X4),
+                    lhsT_scale=w1_planes[a, b][:, rows],
+                    rhs=picked[a][:, cols].bitcast(FP8X4),
+                    rhs_scale=picked_planes[4 * a : P, cols],
+                    start=(a == 0),
+                    stop=(a == K_PASSES - 1),
+                )
+
+        def prepare_w1(a, b, tag, parts):
+            grouped = new_tile([P, PACK, P, PACK], BF16, f"grouped{a}{b}", tag)
+            interleave_w1(nc.scalar.copy, grouped, raw[a, b][:], 0, P)
+            quantise_w1(a, b, grouped, parts)
+
+        source = {}
+        dest = {}
+
+        def pick_sites(b, t, second_copy, tag):
+            h = new_tile([P, S], F32, f"h{b}{t}", tag)
+            nc.scalar.copy(h[:, 0:BANK], banks[b, t, 0][:])
+            second_copy(h[:, BANK:S], banks[b, t, 1][:])
+            last = (b, t) == (BLOCKS - 1, PACK - 1)
+            source[b, t] = new_tile([P, M_OUT], F32, f"source{b}{t}", "x_grouped0" if last else None)
+            nc.vector.tensor_copy(source[b, t][:], h[:].indirect(pos1_sb[:]))
+            dest[b, t] = new_tile([P, M_OUT], F32, f"dest{b}{t}", "x_rows0" if last else None)
+            nc.vector.tensor_copy(dest[b, t][:], h[:].indirect(pos2_sb[:]))
+
+        pick_words(0)
+        nc.vector.tensor_copy(picked_planes[:], tab_planes[:].indirect(offs_sb[:]))
+        prepare_w1(0, 0, "groupedA", 1)
+        for t in range(PACK):
+            first_product(0, 0, t)
+        w2_sorted_planes = new_tile([P, BLOCKS * H], U8, "w2_sorted_planes")
+        nc.vector.tensor_copy(
+            w2_sorted_planes[:].rearrange("p (g t m) -> p g m t", t=PACK, m=P),
+            w2_planes[:].rearrange("p (g m t) -> p g m t", t=PACK, m=P),
+        )
+        pick_words(1)
+        prepare_w1(1, 0, "groupedB", 1)
+        for t in range(PACK):
+            first_product(1, 0, t)
+        pick_words(2)
+        grouped20 = new_tile([P, PACK, P, PACK], BF16, "grouped20")
+        interleave_w1(nc.scalar.copy, grouped20, raw20[0][:], 0, P // 2)
+        interleave_w1(nc.vector.tensor_copy, grouped20, raw20[1][:], P // 2, P // 2)
+        quantise_w1(2, 0, grouped20, PACK)
+        for t in range(PACK):
+            first_product(2, 0, t)
+
+        raw[0, 1] = load_w1(0, K_PASS, K_PASS, "raw01", "rawA")
+        raw[1, 1] = load_w1(1, K_PASS, K_PASS, "raw11", "rawB")
+        raw[2, 1] = load_w1(2, K_PASS, K_PASS, "raw21", "rawC")
+        gain_sb = new_tile([P, BLOCKS, PACK], F32, "gain_sb")
+        nc.sync.dma_start(gain_sb[:], gain.rearrange("(b p t) -> p b t", p=P, t=PACK))
+        skip_sb = new_tile([P, BLOCKS, PACK], F32, "skip_sb")
+        nc.sync.dma_start(skip_sb[:], skip.rearrange("(b p t) -> p b t", p=P, t=PACK))
+        w2_raw = new_tile([P, BLOCKS, H // 2], I32, "w2_raw")
+        nc.sync.dma_start(w2_raw[:], w2_words.bitcast(I32).rearrange("a p c -> p a c"))
+
+        pick_sites(0, 0, nc.vector.tensor_copy, "h00")
+        prepare_w1(0, 1, "groupedA", 1)
+        pick_sites(0, 1, nc.scalar.copy, "rawA")
+        prepare_w1(1, 1, "groupedB", 1)
+        pick_sites(0, 2, nc.scalar.copy, "rawB")
+        prepare_w1(2, 1, "groupedC", PACK)
+        pick_sites(0, 3, nc.scalar.copy, "rawC")
+        for t in range(PACK):
+            for a in range(K_PASSES):
+                first_product(a, 1, t)
+
+        w2_codes = new_tile([P, BLOCKS * 2 * H], U8, "w2_codes", "groupedB")
+        nc.vector.tensor_copy(
+            w2_codes[:].bitcast(U16).rearrange("p (g t m) -> p g m t", t=PACK, m=P),
+            w2_raw[:].rearrange("p a c -> p (a c)").bitcast(U16).rearrange("p (g m t) -> p g m t", t=PACK, m=P),
+        )
+
+        x_rows = [new_tile([P, PACK, M_OUT], BF16, f"x_rows{b}") for b in range(BLOCKS)]
+        x_codes = [new_tile([P, M_OUT], U32, f"x_codes{b}") for b in range(BLOCKS)]
+        x_planes = [new_tile([P, M_OUT], U8, f"x_planes{b}") for b in range(BLOCKS)]
+
+        def activate(b, t):
+            act = new_tile([P, M_OUT], F32, f"act{b}{t}", "groupedC" if b == 0 else f"act{t % 2}")
+            nc.scalar.activation(act[:], source[b, t][:], SILU, bias=silu_bias[:])
+            nc.scalar.activation(x_rows[b][:, t, :], act[:], COPY, scale=gain_sb[:, b, t : t + 1])
+
+        def quantise_x(b):
+            x_grouped = new_tile([P, M_OUT, PACK], BF16, f"x_grouped{b}")
+            nc.vector.tensor_copy(
+                x_grouped[:].rearrange("p (c i) t -> p c t i", i=4),
+                x_rows[b][:].rearrange("p t (c i) -> p c t i", i=4),
+            )
+            nc.vector.quantize_mx(
+                out=x_codes[b][:].bitcast(FP8X4),
+                scales=x_planes[b][:],
+                in_=x_grouped[:].rearrange("p c t -> p (c t)"),
+            )
+
+        for t in range(PACK):
+            activate(0, t)
+            if t == PACK - 1:
+                quantise_x(0)
+            pick_sites(1, t, nc.scalar.copy, f"h1{t}")
+        for t in range(PACK):
+            activate(1, t)
+        quantise_x(1)
+
+        y_banks = [psum.tile([P, BANK], F32, name=f"y_bank{i}", tag=f"bank{i}") for i in range(BLOCKS * PACK)]
+        for a in range(BLOCKS):
+            for i in range(BLOCKS * PACK):
+                c0 = a * H + i * P
+                nc.tensor.matmul_mx(
+                    out=y_banks[i][:],
+                    lhsT=w2_codes[:, 2 * c0 : 2 * (c0 + P)].bitcast(FP4X4),
+                    lhsT_scale=w2_sorted_planes[:, c0 : c0 + P],
+                    rhs=x_codes[a][:].bitcast(FP8X4),
+                    rhs_scale=x_planes[a][:],
+                    start=(a == 0),
+                    stop=(a == BLOCKS - 1),
+                )
+
+        out_rows = out.rearrange("(b p t) m -> b t p m", p=P, t=PACK)
+        for b in range(BLOCKS):
+            for t in range(PACK):
+                result = new_tile([P, M_OUT], F32, f"result{b}{t}", f"source{b}{t}")
+                nc.vector.scalar_tensor_tensor(
+                    result[:], dest[b, t][:], skip_sb[:, b, t : t + 1], y_banks[b * PACK + t][:], MULT, ADD
+                )
+                nc.sync.dma_start(out_rows[b, t], result[:])

@@ -14,7 +14,6 @@ U8 = mybir.dt.uint8
 FP8X4 = mybir.dt.float8_e4m3fn_x4
 FP4X4 = mybir.dt.float4_e2m1fn_x4
 SILU = mybir.ActivationFunctionType.Silu
-COPY = mybir.ActivationFunctionType.Copy
 MULT = mybir.AluOpType.mult
 ADD = mybir.AluOpType.add
 
@@ -43,8 +42,7 @@ def tile_list_ringing_residual_layer_kernel(
         pos2_sb = lists.tile([P, M_OUT // 16], U16, name="pos2_sb")
 
         tab_planes = new_tile([P, T], U8, "tab_planes")
-        nc.vector.memset(tab_planes[:, 0 : T // 2].bitcast(I32), 0)
-        nc.gpsimd.memset(tab_planes[:, T // 2 : T].bitcast(I32), 0)
+        nc.vector.memset(tab_planes[:].bitcast(I32), 0)
         zero = new_tile([P, 1], F32, "zero")
         nc.vector.memset(zero[:], 0.0)
         silu_bias = new_tile([P, 1], F32, "silu_bias")
@@ -66,28 +64,33 @@ def tile_list_ringing_residual_layer_kernel(
         nc.sync.dma_start(offs_sb[:], offs)
         load_tab(0)
         for q in range(4):
-            nc.sync.dma_start(
+            nc.gpsimd.dma_start(
                 tab_planes[32 * q : 32 * q + 4 * K_PASSES, :].bitcast(I32),
                 tab_scales[:, 4 * q : 4 * q + 4, :].bitcast(I32),
             )
+        for q in range(4):
+            nc.gpsimd.dma_start(
+                w2_planes[32 * q : 32 * q + 4, :].bitcast(I32).rearrange("r (a c) -> r a c", a=BLOCKS),
+                w2_scales[:, 4 * q : 4 * q + 4, :].bitcast(I32).rearrange("a r c -> r a c"),
+            )
+        gain_sb = new_tile([P, BLOCKS, PACK], F32, "gain_sb")
+        nc.gpsimd.dma_start(gain_sb[:], gain.rearrange("(b p t) -> p b t", p=P, t=PACK))
+        skip_sb = new_tile([P, BLOCKS, PACK], F32, "skip_sb")
+        nc.gpsimd.dma_start(skip_sb[:], skip.rearrange("(b p t) -> p b t", p=P, t=PACK))
         raw = {}
         raw[0, 0] = load_w1(0, 0, K_PASS, "raw00", "rawA")
         load_tab(1)
         raw[1, 0] = load_w1(1, 0, K_PASS, "raw10", "rawB")
-        for q in range(4):
-            nc.sync.dma_start(
-                w2_planes[32 * q : 32 * q + 4, :].bitcast(I32).rearrange("r (a c) -> r a c", a=BLOCKS),
-                w2_scales[:, 4 * q : 4 * q + 4, :].bitcast(I32).rearrange("a r c -> r a c"),
-            )
         load_tab(2)
         raw20 = [load_w1(2, u * 256, 256, f"raw20_{u}", f"raw20_{u}") for u in range(2)]
         nc.sync.dma_start(pos1_sb[:], pos1)
         nc.sync.dma_start(pos2_sb[:], pos2)
 
-        picked = [new_tile([P, S], U32, f"picked{a}") for a in range(K_PASSES)]
+        picked = {}
         picked_planes = new_tile([P, S], U8, "picked_planes")
 
-        def pick_words(a):
+        def pick_words(a, tag):
+            picked[a] = new_tile([P, S], U32, f"picked{a}", tag)
             nc.vector.tensor_copy(picked[a][:], tab[a][:].bitcast(U32).indirect(offs_sb[:]))
 
         def interleave_w1(copy, grouped, src, m0, count):
@@ -148,7 +151,7 @@ def tile_list_ringing_residual_layer_kernel(
             dest[b, t] = new_tile([P, M_OUT], F32, f"dest{b}{t}", "x_rows0" if last else None)
             nc.vector.tensor_copy(dest[b, t][:], h[:].indirect(pos2_sb[:]))
 
-        pick_words(0)
+        pick_words(0, "picked0")
         nc.vector.tensor_copy(picked_planes[:], tab_planes[:].indirect(offs_sb[:]))
         prepare_w1(0, 0, "groupedA", 1)
         for t in range(PACK):
@@ -158,11 +161,11 @@ def tile_list_ringing_residual_layer_kernel(
             w2_sorted_planes[:].rearrange("p (g t m) -> p g m t", t=PACK, m=P),
             w2_planes[:].rearrange("p (g m t) -> p g m t", t=PACK, m=P),
         )
-        pick_words(1)
+        pick_words(1, "tab_planes")
         prepare_w1(1, 0, "groupedB", 1)
         for t in range(PACK):
             first_product(1, 0, t)
-        pick_words(2)
+        pick_words(2, "w2_planes")
         grouped20 = new_tile([P, PACK, P, PACK], BF16, "grouped20")
         interleave_w1(nc.scalar.copy, grouped20, raw20[0][:], 0, P // 2)
         interleave_w1(nc.vector.tensor_copy, grouped20, raw20[1][:], P // 2, P // 2)
@@ -173,10 +176,6 @@ def tile_list_ringing_residual_layer_kernel(
         raw[0, 1] = load_w1(0, K_PASS, K_PASS, "raw01", "rawA")
         raw[1, 1] = load_w1(1, K_PASS, K_PASS, "raw11", "rawB")
         raw[2, 1] = load_w1(2, K_PASS, K_PASS, "raw21", "rawC")
-        gain_sb = new_tile([P, BLOCKS, PACK], F32, "gain_sb")
-        nc.sync.dma_start(gain_sb[:], gain.rearrange("(b p t) -> p b t", p=P, t=PACK))
-        skip_sb = new_tile([P, BLOCKS, PACK], F32, "skip_sb")
-        nc.sync.dma_start(skip_sb[:], skip.rearrange("(b p t) -> p b t", p=P, t=PACK))
         w2_raw = new_tile([P, BLOCKS, H // 2], I32, "w2_raw")
         nc.sync.dma_start(w2_raw[:], w2_words.bitcast(I32).rearrange("a p c -> p a c"))
 
@@ -204,14 +203,17 @@ def tile_list_ringing_residual_layer_kernel(
         def activate(b, t):
             act = new_tile([P, M_OUT], F32, f"act{b}{t}", "groupedC" if b == 0 else f"act{t % 2}")
             nc.scalar.activation(act[:], source[b, t][:], SILU, bias=silu_bias[:])
-            nc.scalar.activation(x_rows[b][:, t, :], act[:], COPY, scale=gain_sb[:, b, t : t + 1])
+            nc.gpsimd.tensor_scalar(x_rows[b][:, t, :], act[:], gain_sb[:, b, t : t + 1], 0.0, MULT, ADD)
 
-        def quantise_x(b):
+        def quantise_x(b, copies):
             x_grouped = new_tile([P, M_OUT, PACK], BF16, f"x_grouped{b}")
-            nc.vector.tensor_copy(
-                x_grouped[:].rearrange("p (c i) t -> p c t i", i=4),
-                x_rows[b][:].rearrange("p t (c i) -> p c t i", i=4),
-            )
+            width = M_OUT // len(copies)
+            for n, copy in enumerate(copies):
+                cols = slice(n * width, (n + 1) * width)
+                copy(
+                    x_grouped[:, cols, :].rearrange("p (c i) t -> p c t i", i=4),
+                    x_rows[b][:, :, cols].rearrange("p t (c i) -> p c t i", i=4),
+                )
             nc.vector.quantize_mx(
                 out=x_codes[b][:].bitcast(FP8X4),
                 scales=x_planes[b][:],
@@ -221,11 +223,11 @@ def tile_list_ringing_residual_layer_kernel(
         for t in range(PACK):
             activate(0, t)
             if t == PACK - 1:
-                quantise_x(0)
+                quantise_x(0, [nc.scalar.copy])
             pick_sites(1, t, nc.scalar.copy, f"h1{t}")
         for t in range(PACK):
             activate(1, t)
-        quantise_x(1)
+        quantise_x(1, [nc.vector.tensor_copy, nc.scalar.copy])
 
         y_banks = [psum.tile([P, BANK], F32, name=f"y_bank{i}", tag=f"bank{i}") for i in range(BLOCKS * PACK)]
         for a in range(BLOCKS):

@@ -95,8 +95,8 @@ def tile_list_ringing_residual_layer_kernel(
 
         def interleave_w1(copy, grouped, src, m0, count):
             copy(
-                grouped[:, :, m0 : m0 + count, :].rearrange("p t m j -> p m j t"),
-                src.rearrange("p j (m t) -> p m j t", t=PACK),
+                grouped[:, :, m0 : m0 + count, :].rearrange("p (i h) m j -> p i m j h", h=2),
+                src.rearrange("p j (m i h) -> p i m j h", i=2, h=2),
             )
 
         w1_codes = {}
@@ -138,18 +138,27 @@ def tile_list_ringing_residual_layer_kernel(
             interleave_w1(nc.scalar.copy, grouped, raw[a, b][:], 0, P)
             quantise_w1(a, b, grouped, parts)
 
+        h = {}
         source = {}
         dest = {}
 
+        def empty_banks(b, t, second_copy, tag):
+            h[b, t] = new_tile([P, S], F32, f"h{b}{t}", tag)
+            nc.scalar.copy(h[b, t][:, 0:BANK], banks[b, t, 0][:])
+            second_copy(h[b, t][:, BANK:S], banks[b, t, 1][:])
+
+        def pick_source(b, t, picks):
+            source[b, t] = picks
+            nc.vector.tensor_copy(picks, h[b, t][:].indirect(pos1_sb[:]))
+
+        def pick_dest(b, t, picks):
+            dest[b, t] = picks
+            nc.vector.tensor_copy(picks, h[b, t][:].indirect(pos2_sb[:]))
+
         def pick_sites(b, t, second_copy, tag):
-            h = new_tile([P, S], F32, f"h{b}{t}", tag)
-            nc.scalar.copy(h[:, 0:BANK], banks[b, t, 0][:])
-            second_copy(h[:, BANK:S], banks[b, t, 1][:])
-            last = (b, t) == (BLOCKS - 1, PACK - 1)
-            source[b, t] = new_tile([P, M_OUT], F32, f"source{b}{t}", "x_grouped0" if last else None)
-            nc.vector.tensor_copy(source[b, t][:], h[:].indirect(pos1_sb[:]))
-            dest[b, t] = new_tile([P, M_OUT], F32, f"dest{b}{t}", "x_rows0" if last else None)
-            nc.vector.tensor_copy(dest[b, t][:], h[:].indirect(pos2_sb[:]))
+            empty_banks(b, t, second_copy, tag)
+            pick_source(b, t, new_tile([P, M_OUT], F32, f"source{b}{t}")[:])
+            pick_dest(b, t, new_tile([P, M_OUT], F32, f"dest{b}{t}")[:])
 
         pick_words(0, "picked0")
         nc.vector.tensor_copy(picked_planes[:], tab_planes[:].indirect(offs_sb[:]))
@@ -158,8 +167,8 @@ def tile_list_ringing_residual_layer_kernel(
             first_product(0, 0, t)
         w2_sorted_planes = new_tile([P, BLOCKS * H], U8, "w2_sorted_planes")
         nc.vector.tensor_copy(
-            w2_sorted_planes[:].rearrange("p (g t m) -> p g m t", t=PACK, m=P),
-            w2_planes[:].rearrange("p (g m t) -> p g m t", t=PACK, m=P),
+            w2_sorted_planes[:].rearrange("p (g t m) -> p g t m", t=PACK, m=P),
+            w2_planes[:].rearrange("p (g m t) -> p g t m", t=PACK, m=P),
         )
         pick_words(1, "tab_planes")
         prepare_w1(1, 0, "groupedB", 1)
@@ -192,8 +201,8 @@ def tile_list_ringing_residual_layer_kernel(
 
         w2_codes = new_tile([P, BLOCKS * 2 * H], U8, "w2_codes", "groupedB")
         nc.vector.tensor_copy(
-            w2_codes[:].bitcast(U16).rearrange("p (g t m) -> p g m t", t=PACK, m=P),
-            w2_raw[:].rearrange("p a c -> p (a c)").bitcast(U16).rearrange("p (g m t) -> p g m t", t=PACK, m=P),
+            w2_codes[:].bitcast(U16).rearrange("p (g t m) -> p g t m", t=PACK, m=P),
+            w2_raw[:].rearrange("p a c -> p (a c)").bitcast(U16).rearrange("p (g m t) -> p g t m", t=PACK, m=P),
         )
 
         x_rows = [new_tile([P, PACK, M_OUT], BF16, f"x_rows{b}") for b in range(BLOCKS)]
@@ -202,7 +211,7 @@ def tile_list_ringing_residual_layer_kernel(
 
         def activate(b, t):
             act = new_tile([P, M_OUT], F32, f"act{b}{t}", "groupedC" if b == 0 else f"act{t % 2}")
-            nc.scalar.activation(act[:], source[b, t][:], SILU, bias=silu_bias[:])
+            nc.scalar.activation(act[:], source[b, t], SILU, bias=silu_bias[:])
             nc.gpsimd.tensor_scalar(x_rows[b][:, t, :], act[:], gain_sb[:, b, t : t + 1], 0.0, MULT, ADD)
 
         def quantise_x(b, copies):
@@ -220,14 +229,22 @@ def tile_list_ringing_residual_layer_kernel(
                 in_=x_grouped[:].rearrange("p c t -> p (c t)"),
             )
 
-        for t in range(PACK):
+        for t in range(2):
             activate(0, t)
-            if t == PACK - 1:
-                quantise_x(0, [nc.scalar.copy])
             pick_sites(1, t, nc.scalar.copy, f"h1{t}")
+        activate(0, 2)
+        empty_banks(1, 2, nc.scalar.copy, "h12")
+        pick_source(1, 2, new_tile([P, M_OUT], F32, "source12")[:])
+        activate(0, 3)
+        quantise_x(0, [nc.scalar.copy])
+        empty_banks(1, 3, nc.scalar.copy, "h13")
+        last_picks = new_tile([P, 2, M_OUT], F32, "last_picks", "x_grouped0")
+        pick_source(1, 3, last_picks[:, 0, :])
+        pick_dest(1, 3, last_picks[:, 1, :])
         for t in range(PACK):
             activate(1, t)
         quantise_x(1, [nc.vector.tensor_copy, nc.scalar.copy])
+        pick_dest(1, 2, new_tile([P, M_OUT], F32, "dest12", "x_grouped1")[:])
 
         y_banks = [psum.tile([P, BANK], F32, name=f"y_bank{i}", tag=f"bank{i}") for i in range(BLOCKS * PACK)]
         for a in range(BLOCKS):
@@ -247,7 +264,15 @@ def tile_list_ringing_residual_layer_kernel(
         for b in range(BLOCKS):
             for t in range(PACK):
                 result = new_tile([P, M_OUT], F32, f"result{b}{t}", f"source{b}{t}")
-                nc.vector.scalar_tensor_tensor(
-                    result[:], dest[b, t][:], skip_sb[:, b, t : t + 1], y_banks[b * PACK + t][:], MULT, ADD
-                )
-                nc.sync.dma_start(out_rows[b, t], result[:])
+                parts = 2 if (b, t) == (BLOCKS - 1, PACK - 1) else 1
+                for n in range(parts):
+                    cols = slice(n * M_OUT // parts, (n + 1) * M_OUT // parts)
+                    nc.vector.scalar_tensor_tensor(
+                        result[:, cols],
+                        dest[b, t][:, cols],
+                        skip_sb[:, b, t : t + 1],
+                        y_banks[b * PACK + t][:, cols],
+                        MULT,
+                        ADD,
+                    )
+                    nc.sync.dma_start(out_rows[b, t][:, cols], result[:, cols])

@@ -51,61 +51,78 @@ def tile_list_ringing_residual_layer_kernel(
         nc.vector.memset(w2_planes[:].bitcast(I32), 0)
 
         tab = [new_tile([P, T], I32, f"tab{a}") for a in range(K_PASSES)]
+        raw = {}
 
         def load_tab(a):
             nc.sync.dma_start(tab[a][:], tab_words[a].rearrange("p t i -> p (t i)").bitcast(I32))
 
-        def load_w1(a, c0, width, name, tag):
-            raw = new_tile([P, PACK, width], F32, name, tag)
-            rows = w1[a * K_PASS : (a + 1) * K_PASS, c0 : c0 + width]
-            nc.sync.dma_start(raw[:], rows.rearrange("(p j) c -> p j c", j=PACK))
-            return raw
+        def load_w1(a, b):
+            raw[a, b] = new_tile([P, PACK, K_PASS], F32, f"raw{a}{b}")
+            rows = w1[a * K_PASS : (a + 1) * K_PASS, b * K_PASS : (b + 1) * K_PASS]
+            nc.sync.dma_start(raw[a, b][:], rows.rearrange("(p j) c -> p j c", j=PACK))
 
         nc.sync.dma_start(offs_sb[:], offs)
+        load_w1(0, 0)
         load_tab(0)
         for q in range(4):
             nc.gpsimd.dma_start(
                 tab_planes[32 * q : 32 * q + 4 * K_PASSES, :].bitcast(I32),
                 tab_scales[:, 4 * q : 4 * q + 4, :].bitcast(I32),
             )
+        load_w1(2, 0)
+        load_tab(1)
+        load_w1(1, 0)
         for q in range(4):
             nc.gpsimd.dma_start(
                 w2_planes[32 * q : 32 * q + 4, :].bitcast(I32).rearrange("r (a c) -> r a c", a=BLOCKS),
                 w2_scales[:, 4 * q : 4 * q + 4, :].bitcast(I32).rearrange("a r c -> r a c"),
             )
+        load_tab(2)
+        nc.sync.dma_start(pos1_sb[:], pos1)
+        load_w1(0, 1)
+        nc.sync.dma_start(pos2_sb[:], pos2)
+        load_w1(1, 1)
         gain_sb = new_tile([P, BLOCKS, PACK], F32, "gain_sb")
         nc.gpsimd.dma_start(gain_sb[:], gain.rearrange("(b p t) -> p b t", p=P, t=PACK))
+        load_w1(2, 1)
         skip_sb = new_tile([P, BLOCKS, PACK], F32, "skip_sb")
         nc.gpsimd.dma_start(skip_sb[:], skip.rearrange("(b p t) -> p b t", p=P, t=PACK))
-        raw = {}
-        raw[0, 0] = load_w1(0, 0, K_PASS, "raw00", "rawA")
-        load_tab(1)
-        raw[1, 0] = load_w1(1, 0, K_PASS, "raw10", "rawB")
-        load_tab(2)
-        raw20 = [load_w1(2, u * 256, 256, f"raw20_{u}", f"raw20_{u}") for u in range(2)]
-        nc.sync.dma_start(pos1_sb[:], pos1)
-        nc.sync.dma_start(pos2_sb[:], pos2)
+        w2_raw = new_tile([P, BLOCKS, H // 2], I32, "w2_raw")
+        nc.sync.dma_start(w2_raw[:], w2_words.bitcast(I32).rearrange("a p c -> p a c"))
 
         picked = {}
         picked_planes = new_tile([P, S], U8, "picked_planes")
 
-        def pick_words(a, tag):
-            picked[a] = new_tile([P, S], U32, f"picked{a}", tag)
-            nc.vector.tensor_copy(picked[a][:], tab[a][:].bitcast(U32).indirect(offs_sb[:]))
+        def pick_words(a):
+            words = new_tile([P, S], U32, f"picked{a}")
+            nc.vector.tensor_copy(words[:], tab[a][:].bitcast(U32).indirect(offs_sb[:]))
+            for u in range(2):
+                picked[a, u] = words[:, u * BANK : (u + 1) * BANK]
 
-        def interleave_w1(copy, grouped, src, m0, count):
-            copy(
-                grouped[:, :, m0 : m0 + count, :].rearrange("p (i h) m j -> p i m j h", h=2),
-                src.rearrange("p j (m i h) -> p i m j h", i=2, h=2),
-            )
+        def pick_words_half(a, u, tag):
+            words = new_tile([P, BANK], U32, f"picked{a}{u}", tag)
+            entries = offs_sb[:, u * BANK // 16 : (u + 1) * BANK // 16]
+            nc.vector.tensor_copy(words[:], tab[a][:].bitcast(U32).indirect(entries))
+            picked[a, u] = words[:]
 
+        grouped = {}
         w1_codes = {}
         w1_planes = {}
 
-        def quantise_w1(a, b, grouped, parts):
+        def interleave_w1(a, b, copies):
+            grouped[a, b] = new_tile([P, PACK, P, PACK], BF16, f"grouped{a}{b}")
+            count = P // len(copies)
+            for n, copy in enumerate(copies):
+                m0 = n * count
+                copy(
+                    grouped[a, b][:, :, m0 : m0 + count, :].rearrange("p (i h) m j -> p i m j h", h=2),
+                    raw[a, b][:, :, PACK * m0 : PACK * (m0 + count)].rearrange("p j (m i h) -> p i m j h", i=2, h=2),
+                )
+
+        def quantise_w1(a, b, parts):
             w1_codes[a, b] = new_tile([P, K_PASS], U32, f"w1_codes{a}{b}")
             w1_planes[a, b] = new_tile([P, K_PASS], U8, f"w1_planes{a}{b}")
-            flat = grouped[:].rearrange("p t m j -> p (t m j)")
+            flat = grouped[a, b][:].rearrange("p t m j -> p (t m j)")
             width = K_PASS // parts
             for i in range(parts):
                 cols = slice(i * width, (i + 1) * width)
@@ -127,92 +144,83 @@ def tile_list_ringing_residual_layer_kernel(
                     out=banks[b, t, u][:],
                     lhsT=w1_codes[a, b][:, rows].bitcast(FP8X4),
                     lhsT_scale=w1_planes[a, b][:, rows],
-                    rhs=picked[a][:, cols].bitcast(FP8X4),
+                    rhs=picked[a, u].bitcast(FP8X4),
                     rhs_scale=picked_planes[4 * a : P, cols],
                     start=(a == 0),
                     stop=(a == K_PASSES - 1),
                 )
 
-        def prepare_w1(a, b, tag, parts):
-            grouped = new_tile([P, PACK, P, PACK], BF16, f"grouped{a}{b}", tag)
-            interleave_w1(nc.scalar.copy, grouped, raw[a, b][:], 0, P)
-            quantise_w1(a, b, grouped, parts)
-
-        h = {}
+        h = [new_tile([P, PACK, S], F32, f"h{b}", f"tab{b}") for b in range(BLOCKS)]
         source = {}
         dest = {}
 
-        def empty_banks(b, t, second_copy, tag):
-            h[b, t] = new_tile([P, S], F32, f"h{b}{t}", tag)
-            nc.scalar.copy(h[b, t][:, 0:BANK], banks[b, t, 0][:])
-            second_copy(h[b, t][:, BANK:S], banks[b, t, 1][:])
+        def empty_banks(b, t):
+            for u in range(2):
+                nc.scalar.copy(h[b][:, t, u * BANK : (u + 1) * BANK], banks[b, t, u][:])
 
-        def pick_source(b, t, picks):
-            source[b, t] = picks
-            nc.vector.tensor_copy(picks, h[b, t][:].indirect(pos1_sb[:]))
+        def pick_source(b, t):
+            source[b, t] = new_tile([P, M_OUT], F32, f"source{b}{t}")
+            nc.vector.tensor_copy(source[b, t][:], h[b][:, t, :].indirect(pos1_sb[:]))
 
         def pick_dest(b, t, picks):
             dest[b, t] = picks
-            nc.vector.tensor_copy(picks, h[b, t][:].indirect(pos2_sb[:]))
+            nc.vector.tensor_copy(picks, h[b][:, t, :].indirect(pos2_sb[:]))
 
-        def pick_sites(b, t, second_copy, tag):
-            empty_banks(b, t, second_copy, tag)
-            pick_source(b, t, new_tile([P, M_OUT], F32, f"source{b}{t}")[:])
-            pick_dest(b, t, new_tile([P, M_OUT], F32, f"dest{b}{t}")[:])
-
-        pick_words(0, "picked0")
+        interleave_w1(0, 0, [nc.scalar.copy])
+        quantise_w1(0, 0, 1)
         nc.vector.tensor_copy(picked_planes[:], tab_planes[:].indirect(offs_sb[:]))
-        prepare_w1(0, 0, "groupedA", 1)
+        pick_words(0)
         for t in range(PACK):
             first_product(0, 0, t)
+        interleave_w1(2, 0, [nc.scalar.copy])
+        quantise_w1(2, 0, 1)
         w2_sorted_planes = new_tile([P, BLOCKS * H], U8, "w2_sorted_planes")
         nc.vector.tensor_copy(
             w2_sorted_planes[:].rearrange("p (g t m) -> p g t m", t=PACK, m=P),
             w2_planes[:].rearrange("p (g m t) -> p g t m", t=PACK, m=P),
         )
-        pick_words(1, "tab_planes")
-        prepare_w1(1, 0, "groupedB", 1)
+        pick_words(1)
+        interleave_w1(1, 0, [nc.scalar.copy])
+        quantise_w1(1, 0, 1)
         for t in range(PACK):
             first_product(1, 0, t)
-        pick_words(2, "w2_planes")
-        grouped20 = new_tile([P, PACK, P, PACK], BF16, "grouped20")
-        interleave_w1(nc.scalar.copy, grouped20, raw20[0][:], 0, P // 2)
-        interleave_w1(nc.vector.tensor_copy, grouped20, raw20[1][:], P // 2, P // 2)
-        quantise_w1(2, 0, grouped20, PACK)
+        pick_words_half(2, 0, "tab_planes")
+        pick_words_half(2, 1, "w2_planes")
         for t in range(PACK):
             first_product(2, 0, t)
+            empty_banks(0, t)
+        for t in range(PACK):
+            pick_source(0, t)
 
-        raw[0, 1] = load_w1(0, K_PASS, K_PASS, "raw01", "rawA")
-        raw[1, 1] = load_w1(1, K_PASS, K_PASS, "raw11", "rawB")
-        raw[2, 1] = load_w1(2, K_PASS, K_PASS, "raw21", "rawC")
-        w2_raw = new_tile([P, BLOCKS, H // 2], I32, "w2_raw")
-        nc.sync.dma_start(w2_raw[:], w2_words.bitcast(I32).rearrange("a p c -> p a c"))
-
-        pick_sites(0, 0, nc.vector.tensor_copy, "h00")
-        prepare_w1(0, 1, "groupedA", 1)
-        pick_sites(0, 1, nc.scalar.copy, "rawA")
-        prepare_w1(1, 1, "groupedB", 1)
-        pick_sites(0, 2, nc.scalar.copy, "rawB")
-        prepare_w1(2, 1, "groupedC", PACK)
-        pick_sites(0, 3, nc.scalar.copy, "rawC")
+        interleave_w1(0, 1, [nc.scalar.copy])
+        quantise_w1(0, 1, 1)
+        interleave_w1(1, 1, [nc.scalar.copy])
+        quantise_w1(1, 1, 1)
+        interleave_w1(2, 1, [nc.vector.tensor_copy, nc.scalar.copy])
+        quantise_w1(2, 1, PACK)
         for t in range(PACK):
             for a in range(K_PASSES):
                 first_product(a, 1, t)
+        for t in range(PACK):
+            empty_banks(1, t)
+            pick_source(1, t)
 
-        w2_codes = new_tile([P, BLOCKS * 2 * H], U8, "w2_codes", "groupedB")
+        w2_codes = new_tile([P, BLOCKS * 2 * H], U8, "w2_codes", "grouped21")
         nc.vector.tensor_copy(
             w2_codes[:].bitcast(U16).rearrange("p (g t m) -> p g t m", t=PACK, m=P),
             w2_raw[:].rearrange("p a c -> p (a c)").bitcast(U16).rearrange("p (g m t) -> p g t m", t=PACK, m=P),
         )
+        for t, tag in enumerate(["dest00", "grouped01", "grouped11", "w2_raw"]):
+            pick_dest(0, t, new_tile([P, M_OUT], F32, f"dest0{t}", tag)[:])
 
+        act = [new_tile([P, PACK, M_OUT], F32, f"act{b}", f"raw1{1 - b}") for b in range(BLOCKS)]
         x_rows = [new_tile([P, PACK, M_OUT], BF16, f"x_rows{b}") for b in range(BLOCKS)]
         x_codes = [new_tile([P, M_OUT], U32, f"x_codes{b}") for b in range(BLOCKS)]
         x_planes = [new_tile([P, M_OUT], U8, f"x_planes{b}") for b in range(BLOCKS)]
 
         def activate(b, t):
-            act = new_tile([P, M_OUT], F32, f"act{b}{t}", "groupedC" if b == 0 else f"act{t % 2}")
-            nc.scalar.activation(act[:], source[b, t], SILU, bias=silu_bias[:])
-            nc.gpsimd.tensor_scalar(x_rows[b][:, t, :], act[:], gain_sb[:, b, t : t + 1], 0.0, MULT, ADD)
+            nc.scalar.activation(act[b][:, t, :], source[b, t][:], SILU, bias=silu_bias[:])
+            nc.gpsimd.tensor_scalar(x_rows[b][:, t, :], act[b][:, t, :], gain_sb[:, b, t : t + 1], 0.0, MULT, ADD)
 
         def quantise_x(b, copies):
             x_grouped = new_tile([P, M_OUT, PACK], BF16, f"x_grouped{b}")
@@ -229,22 +237,17 @@ def tile_list_ringing_residual_layer_kernel(
                 in_=x_grouped[:].rearrange("p c t -> p (c t)"),
             )
 
-        for t in range(2):
+        for t in range(PACK):
             activate(0, t)
-            pick_sites(1, t, nc.scalar.copy, f"h1{t}")
-        activate(0, 2)
-        empty_banks(1, 2, nc.scalar.copy, "h12")
-        pick_source(1, 2, new_tile([P, M_OUT], F32, "source12")[:])
-        activate(0, 3)
         quantise_x(0, [nc.scalar.copy])
-        empty_banks(1, 3, nc.scalar.copy, "h13")
-        last_picks = new_tile([P, 2, M_OUT], F32, "last_picks", "x_grouped0")
-        pick_source(1, 3, last_picks[:, 0, :])
-        pick_dest(1, 3, last_picks[:, 1, :])
         for t in range(PACK):
             activate(1, t)
         quantise_x(1, [nc.vector.tensor_copy, nc.scalar.copy])
-        pick_dest(1, 2, new_tile([P, M_OUT], F32, "dest12", "x_grouped1")[:])
+        for t in range(2):
+            pick_dest(1, t, new_tile([P, M_OUT], F32, f"dest1{t}", f"source1{t + 2}")[:])
+        last_picks = new_tile([P, 2, M_OUT], F32, "last_picks", "x_grouped1")
+        for t in range(2):
+            pick_dest(1, t + 2, last_picks[:, t, :])
 
         y_banks = [psum.tile([P, BANK], F32, name=f"y_bank{i}", tag=f"bank{i}") for i in range(BLOCKS * PACK)]
         for a in range(BLOCKS):
@@ -262,17 +265,17 @@ def tile_list_ringing_residual_layer_kernel(
 
         out_rows = out.rearrange("(b p t) m -> b t p m", p=P, t=PACK)
         for b in range(BLOCKS):
+            result = new_tile([P, PACK, M_OUT], F32, f"result{b}", f"raw{2 * b}0")
             for t in range(PACK):
-                result = new_tile([P, M_OUT], F32, f"result{b}{t}", f"source{b}{t}")
                 parts = 2 if (b, t) == (BLOCKS - 1, PACK - 1) else 1
                 for n in range(parts):
                     cols = slice(n * M_OUT // parts, (n + 1) * M_OUT // parts)
                     nc.vector.scalar_tensor_tensor(
-                        result[:, cols],
+                        result[:, t, cols],
                         dest[b, t][:, cols],
                         skip_sb[:, b, t : t + 1],
                         y_banks[b * PACK + t][:, cols],
                         MULT,
                         ADD,
                     )
-                    nc.sync.dma_start(out_rows[b, t][:, cols], result[:, cols])
+                    nc.sync.dma_start(out_rows[b, t][:, cols], result[:, t, cols])

@@ -105,6 +105,9 @@ def tile_list_ringing_residual_layer_kernel(
             nc.vector.tensor_copy(words[:], tab[a][:].bitcast(U32).indirect(entries))
             picked[a, u] = words[:]
 
+        def gpsimd_copy(dst, src):
+            nc.gpsimd.tensor_scalar(dst, src, 1.0, 0.0, MULT, ADD)
+
         grouped = {}
         w1_codes = {}
         w1_planes = {}
@@ -119,8 +122,16 @@ def tile_list_ringing_residual_layer_kernel(
                     raw[a, b][:, :, PACK * m0 : PACK * (m0 + count)].rearrange("p j (m i h) -> p i m j h", i=2, h=2),
                 )
 
-        def quantise_w1(a, b, parts):
-            w1_codes[a, b] = new_tile([P, K_PASS], U32, f"w1_codes{a}{b}")
+        def interleave_w1_gpsimd(a, b):
+            grouped[a, b] = new_tile([P, PACK, P, PACK], BF16, f"grouped{a}{b}")
+            for i in range(2):
+                gpsimd_copy(
+                    grouped[a, b][:, 2 * i : 2 * i + 2].rearrange("p h m j -> p m j h"),
+                    raw[a, b][:].rearrange("p j (m i h) -> p i m j h", i=2, h=2)[:, i],
+                )
+
+        def quantise_w1(a, b, parts, tag=None):
+            w1_codes[a, b] = new_tile([P, K_PASS], U32, f"w1_codes{a}{b}", tag)
             w1_planes[a, b] = new_tile([P, K_PASS], U8, f"w1_planes{a}{b}")
             flat = grouped[a, b][:].rearrange("p t m j -> p (t m j)")
             width = K_PASS // parts
@@ -134,9 +145,9 @@ def tile_list_ringing_residual_layer_kernel(
 
         banks = {}
 
-        def first_product(a, b, t):
+        def first_product(order, a, b, t):
             for u in range(2):
-                if a == 0:
+                if a == order[0]:
                     banks[b, t, u] = psum.tile([P, BANK], F32, name=f"h_bank{b}{t}{u}", tag=f"bank{2 * t + u}")
                 rows = slice(t * P, (t + 1) * P)
                 cols = slice(u * BANK, (u + 1) * BANK)
@@ -146,8 +157,8 @@ def tile_list_ringing_residual_layer_kernel(
                     lhsT_scale=w1_planes[a, b][:, rows],
                     rhs=picked[a, u].bitcast(FP8X4),
                     rhs_scale=picked_planes[4 * a : P, cols],
-                    start=(a == 0),
-                    stop=(a == K_PASSES - 1),
+                    start=(a == order[0]),
+                    stop=(a == order[-1]),
                 )
 
         h = [new_tile([P, PACK, S], F32, f"h{b}", f"tab{b}") for b in range(BLOCKS)]
@@ -171,7 +182,7 @@ def tile_list_ringing_residual_layer_kernel(
         nc.vector.tensor_copy(picked_planes[:], tab_planes[:].indirect(offs_sb[:]))
         pick_words(0)
         for t in range(PACK):
-            first_product(0, 0, t)
+            first_product((0, 1, 2), 0, 0, t)
         interleave_w1(2, 0, [nc.scalar.copy])
         quantise_w1(2, 0, 1)
         w2_sorted_planes = new_tile([P, BLOCKS * H], U8, "w2_sorted_planes")
@@ -183,34 +194,35 @@ def tile_list_ringing_residual_layer_kernel(
         interleave_w1(1, 0, [nc.scalar.copy])
         quantise_w1(1, 0, 1)
         for t in range(PACK):
-            first_product(1, 0, t)
+            first_product((0, 1, 2), 1, 0, t)
         pick_words_half(2, 0, "tab_planes")
         pick_words_half(2, 1, "w2_planes")
         for t in range(PACK):
-            first_product(2, 0, t)
+            first_product((0, 1, 2), 2, 0, t)
             empty_banks(0, t)
         for t in range(PACK):
             pick_source(0, t)
 
-        interleave_w1(0, 1, [nc.scalar.copy])
-        quantise_w1(0, 1, 1)
+        interleave_w1_gpsimd(0, 1)
         interleave_w1(1, 1, [nc.scalar.copy])
         quantise_w1(1, 1, 1)
-        interleave_w1(2, 1, [nc.vector.tensor_copy, nc.scalar.copy])
-        quantise_w1(2, 1, PACK)
+        interleave_w1(2, 1, [nc.scalar.copy])
+        quantise_w1(2, 1, 1)
+        quantise_w1(0, 1, PACK, "grouped21")
+        order = (1, 2, 0)
         for t in range(PACK):
-            for a in range(K_PASSES):
-                first_product(a, 1, t)
+            for a in order:
+                first_product(order, a, 1, t)
         for t in range(PACK):
             empty_banks(1, t)
             pick_source(1, t)
 
-        w2_codes = new_tile([P, BLOCKS * 2 * H], U8, "w2_codes", "grouped21")
+        w2_codes = new_tile([P, BLOCKS * 2 * H], U8, "w2_codes", "grouped01")
         nc.vector.tensor_copy(
             w2_codes[:].bitcast(U16).rearrange("p (g t m) -> p g t m", t=PACK, m=P),
             w2_raw[:].rearrange("p a c -> p (a c)").bitcast(U16).rearrange("p (g m t) -> p g t m", t=PACK, m=P),
         )
-        for t, tag in enumerate(["dest00", "grouped01", "grouped11", "w2_raw"]):
+        for t, tag in enumerate(["dest00", "dest01", "grouped11", "w2_raw"]):
             pick_dest(0, t, new_tile([P, M_OUT], F32, f"dest0{t}", tag)[:])
 
         act = [new_tile([P, PACK, M_OUT], F32, f"act{b}", f"raw1{1 - b}") for b in range(BLOCKS)]
@@ -239,7 +251,7 @@ def tile_list_ringing_residual_layer_kernel(
 
         for t in range(PACK):
             activate(0, t)
-        quantise_x(0, [nc.scalar.copy])
+        quantise_x(0, [gpsimd_copy])
         for t in range(PACK):
             activate(1, t)
         quantise_x(1, [nc.vector.tensor_copy, nc.scalar.copy])

@@ -14,6 +14,7 @@ U8 = mybir.dt.uint8
 FP8X4 = mybir.dt.float8_e4m3fn_x4
 FP4X4 = mybir.dt.float4_e2m1fn_x4
 SILU = mybir.ActivationFunctionType.Silu
+COPY = mybir.ActivationFunctionType.Copy
 MULT = mybir.AluOpType.mult
 ADD = mybir.AluOpType.add
 
@@ -62,31 +63,35 @@ def tile_list_ringing_residual_layer_kernel(
             nc.sync.dma_start(raw[a, b][:], rows.rearrange("(p j) c -> p j c", j=PACK))
 
         nc.sync.dma_start(offs_sb[:], offs)
-        load_w1(0, 0)
         load_tab(0)
+        load_w1(0, 0)
         for q in range(4):
-            nc.gpsimd.dma_start(
-                tab_planes[32 * q : 32 * q + 4 * K_PASSES, :].bitcast(I32),
+            nc.sync.dma_start(
+                tab_planes[32 * q + 4 : 32 * q + 4 + 4 * K_PASSES, :].bitcast(I32),
                 tab_scales[:, 4 * q : 4 * q + 4, :].bitcast(I32),
             )
-        load_w1(2, 0)
         load_tab(1)
         load_w1(1, 0)
         for q in range(4):
-            nc.gpsimd.dma_start(
+            nc.sync.dma_start(
                 w2_planes[32 * q : 32 * q + 4, :].bitcast(I32).rearrange("r (a c) -> r a c", a=BLOCKS),
                 w2_scales[:, 4 * q : 4 * q + 4, :].bitcast(I32).rearrange("a r c -> r a c"),
             )
         load_tab(2)
+        half = K_PASS // 2
+        raw20 = [new_tile([P, PACK, half], F32, f"raw20_{n}") for n in range(2)]
+        for n in range(2):
+            rows = w1[2 * K_PASS : 3 * K_PASS, n * half : (n + 1) * half]
+            nc.sync.dma_start(raw20[n][:], rows.rearrange("(p j) c -> p j c", j=PACK))
         nc.sync.dma_start(pos1_sb[:], pos1)
         load_w1(0, 1)
         nc.sync.dma_start(pos2_sb[:], pos2)
         load_w1(1, 1)
         gain_sb = new_tile([P, BLOCKS, PACK], F32, "gain_sb")
-        nc.gpsimd.dma_start(gain_sb[:], gain.rearrange("(b p t) -> p b t", p=P, t=PACK))
+        nc.sync.dma_start(gain_sb[:], gain.rearrange("(b p t) -> p b t", p=P, t=PACK))
         load_w1(2, 1)
         skip_sb = new_tile([P, BLOCKS, PACK], F32, "skip_sb")
-        nc.gpsimd.dma_start(skip_sb[:], skip.rearrange("(b p t) -> p b t", p=P, t=PACK))
+        nc.sync.dma_start(skip_sb[:], skip.rearrange("(b p t) -> p b t", p=P, t=PACK))
         w2_raw = new_tile([P, BLOCKS, H // 2], I32, "w2_raw")
         nc.sync.dma_start(w2_raw[:], w2_words.bitcast(I32).rearrange("a p c -> p a c"))
 
@@ -105,33 +110,22 @@ def tile_list_ringing_residual_layer_kernel(
             nc.vector.tensor_copy(words[:], tab[a][:].bitcast(U32).indirect(entries))
             picked[a, u] = words[:]
 
-        def gpsimd_copy(dst, src):
-            nc.gpsimd.tensor_scalar(dst, src, 1.0, 0.0, MULT, ADD)
-
         grouped = {}
         w1_codes = {}
         w1_planes = {}
 
-        def interleave_w1(a, b, copies):
-            grouped[a, b] = new_tile([P, PACK, P, PACK], BF16, f"grouped{a}{b}")
-            count = P // len(copies)
-            for n, copy in enumerate(copies):
-                m0 = n * count
-                copy(
-                    grouped[a, b][:, :, m0 : m0 + count, :].rearrange("p (i h) m j -> p i m j h", h=2),
-                    raw[a, b][:, :, PACK * m0 : PACK * (m0 + count)].rearrange("p j (m i h) -> p i m j h", i=2, h=2),
-                )
+        def interleave(copy, dst, src, m0, count):
+            copy(
+                dst[:, :, m0 : m0 + count, :].rearrange("p (i h) m j -> p i m j h", h=2),
+                src.rearrange("p j (m i h) -> p i m j h", i=2, h=2),
+            )
 
-        def interleave_w1_gpsimd(a, b):
-            grouped[a, b] = new_tile([P, PACK, P, PACK], BF16, f"grouped{a}{b}")
-            for i in range(2):
-                gpsimd_copy(
-                    grouped[a, b][:, 2 * i : 2 * i + 2].rearrange("p h m j -> p m j h"),
-                    raw[a, b][:].rearrange("p j (m i h) -> p i m j h", i=2, h=2)[:, i],
-                )
+        def interleave_w1(copy, a, b, tag=None):
+            grouped[a, b] = new_tile([P, PACK, P, PACK], BF16, f"grouped{a}{b}", tag)
+            interleave(copy, grouped[a, b], raw[a, b][:], 0, P)
 
-        def quantise_w1(a, b, parts, tag=None):
-            w1_codes[a, b] = new_tile([P, K_PASS], U32, f"w1_codes{a}{b}", tag)
+        def quantise_w1(a, b, parts):
+            w1_codes[a, b] = new_tile([P, K_PASS], U32, f"w1_codes{a}{b}")
             w1_planes[a, b] = new_tile([P, K_PASS], U8, f"w1_planes{a}{b}")
             flat = grouped[a, b][:].rearrange("p t m j -> p (t m j)")
             width = K_PASS // parts
@@ -145,9 +139,9 @@ def tile_list_ringing_residual_layer_kernel(
 
         banks = {}
 
-        def first_product(order, a, b, t):
+        def first_product(a, b, t):
             for u in range(2):
-                if a == order[0]:
+                if a == 0:
                     banks[b, t, u] = psum.tile([P, BANK], F32, name=f"h_bank{b}{t}{u}", tag=f"bank{2 * t + u}")
                 rows = slice(t * P, (t + 1) * P)
                 cols = slice(u * BANK, (u + 1) * BANK)
@@ -156,12 +150,12 @@ def tile_list_ringing_residual_layer_kernel(
                     lhsT=w1_codes[a, b][:, rows].bitcast(FP8X4),
                     lhsT_scale=w1_planes[a, b][:, rows],
                     rhs=picked[a, u].bitcast(FP8X4),
-                    rhs_scale=picked_planes[4 * a : P, cols],
-                    start=(a == order[0]),
-                    stop=(a == order[-1]),
+                    rhs_scale=picked_planes[4 * (a + 1) : P, cols],
+                    start=(a == 0),
+                    stop=(a == K_PASSES - 1),
                 )
 
-        h = [new_tile([P, PACK, S], F32, f"h{b}", f"tab{b}") for b in range(BLOCKS)]
+        h = [new_tile([P, PACK, S], F32, "h0", "tab0")]
         source = {}
         dest = {}
 
@@ -170,96 +164,112 @@ def tile_list_ringing_residual_layer_kernel(
                 nc.scalar.copy(h[b][:, t, u * BANK : (u + 1) * BANK], banks[b, t, u][:])
 
         def pick_source(b, t):
-            source[b, t] = new_tile([P, M_OUT], F32, f"source{b}{t}")
+            source[b, t] = new_tile([P, M_OUT], F32, f"source{b}{t}", {(0, 0): "grouped01", (0, 3): "tab1"}.get((b, t)))
             nc.vector.tensor_copy(source[b, t][:], h[b][:, t, :].indirect(pos1_sb[:]))
 
         def pick_dest(b, t, picks):
             dest[b, t] = picks
             nc.vector.tensor_copy(picks, h[b][:, t, :].indirect(pos2_sb[:]))
 
-        interleave_w1(0, 0, [nc.scalar.copy])
-        quantise_w1(0, 0, 1)
-        nc.vector.tensor_copy(picked_planes[:], tab_planes[:].indirect(offs_sb[:]))
         pick_words(0)
+        nc.vector.tensor_copy(picked_planes[:], tab_planes[:].indirect(offs_sb[:]))
+        interleave_w1(nc.scalar.copy, 0, 0)
+        quantise_w1(0, 0, 1)
         for t in range(PACK):
-            first_product((0, 1, 2), 0, 0, t)
-        interleave_w1(2, 0, [nc.scalar.copy])
-        quantise_w1(2, 0, 1)
+            first_product(0, 0, t)
+        pick_words(1)
+        interleave_w1(nc.scalar.copy, 1, 0)
+        quantise_w1(1, 0, 1)
+        for t in range(PACK):
+            first_product(1, 0, t)
         w2_sorted_planes = new_tile([P, BLOCKS * H], U8, "w2_sorted_planes")
         nc.vector.tensor_copy(
             w2_sorted_planes[:].rearrange("p (g t m) -> p g t m", t=PACK, m=P),
             w2_planes[:].rearrange("p (g m t) -> p g t m", t=PACK, m=P),
         )
-        pick_words(1)
-        interleave_w1(1, 0, [nc.scalar.copy])
-        quantise_w1(1, 0, 1)
-        for t in range(PACK):
-            first_product((0, 1, 2), 1, 0, t)
         pick_words_half(2, 0, "tab_planes")
         pick_words_half(2, 1, "w2_planes")
+        grouped[2, 0] = new_tile([P, PACK, P, PACK], BF16, "grouped20")
+        interleave(nc.scalar.copy, grouped[2, 0], raw20[0][:], 0, P // 2)
+        interleave(nc.vector.tensor_copy, grouped[2, 0], raw20[1][:], P // 2, P // 2)
+        quantise_w1(2, 0, PACK)
         for t in range(PACK):
-            first_product((0, 1, 2), 2, 0, t)
+            first_product(2, 0, t)
             empty_banks(0, t)
+        interleave_w1(nc.vector.tensor_copy, 0, 1)
+        quantise_w1(0, 1, 1)
         for t in range(PACK):
             pick_source(0, t)
 
-        interleave_w1_gpsimd(0, 1)
-        interleave_w1(1, 1, [nc.scalar.copy])
+        interleave_w1(nc.scalar.copy, 1, 1, "w1_codes20")
         quantise_w1(1, 1, 1)
-        interleave_w1(2, 1, [nc.scalar.copy])
-        quantise_w1(2, 1, 1)
-        quantise_w1(0, 1, PACK, "grouped21")
-        order = (1, 2, 0)
+        interleave_w1(nc.scalar.copy, 2, 1)
+        quantise_w1(2, 1, 2)
         for t in range(PACK):
-            for a in order:
-                first_product(order, a, 1, t)
+            for a in range(K_PASSES):
+                first_product(a, 1, t)
+        act = [new_tile([P, PACK, M_OUT], F32, "act0", "raw21")]
+        x_rows = [new_tile([P, PACK, M_OUT], BF16, f"x_rows{b}") for b in range(BLOCKS)]
+        x_codes = [new_tile([P, M_OUT], U32, f"x_codes{b}", ["x_rows0", None][b]) for b in range(BLOCKS)]
+        x_planes = [new_tile([P, M_OUT], U8, f"x_planes{b}") for b in range(BLOCKS)]
+
+        def activate(b, t):
+            silu = act[b][:, t, :]
+            nc.scalar.activation(silu, source[b, t][:], SILU, bias=silu_bias[:])
+            if (b, t) == (BLOCKS - 1, PACK - 1):
+                nc.scalar.activation(x_rows[b][:, t, :], silu, COPY, scale=gain_sb[:, b, t : t + 1])
+            else:
+                nc.gpsimd.tensor_scalar(x_rows[b][:, t, :], silu, gain_sb[:, b, t : t + 1], 0.0, MULT, ADD)
+
+        for t in range(PACK):
+            activate(0, t)
+        h.append(new_tile([P, PACK, S], F32, "h1", "tab1"))
         for t in range(PACK):
             empty_banks(1, t)
             pick_source(1, t)
 
-        w2_codes = new_tile([P, BLOCKS * 2 * H], U8, "w2_codes", "grouped01")
+        w2_codes = new_tile([P, BLOCKS * 2 * H], U8, "w2_codes", "grouped21")
         nc.vector.tensor_copy(
             w2_codes[:].bitcast(U16).rearrange("p (g t m) -> p g t m", t=PACK, m=P),
             w2_raw[:].rearrange("p a c -> p (a c)").bitcast(U16).rearrange("p (g m t) -> p g t m", t=PACK, m=P),
         )
-        for t, tag in enumerate(["dest00", "dest01", "grouped11", "w2_raw"]):
-            pick_dest(0, t, new_tile([P, M_OUT], F32, f"dest0{t}", tag)[:])
+        pick_dest(0, 0, new_tile([P, M_OUT], F32, "dest00", "w1_codes20")[:])
+        pick_dest(0, 1, new_tile([P, M_OUT], F32, "dest01", "w2_raw")[:])
 
-        act = [new_tile([P, PACK, M_OUT], F32, f"act{b}", f"raw1{1 - b}") for b in range(BLOCKS)]
-        x_rows = [new_tile([P, PACK, M_OUT], BF16, f"x_rows{b}") for b in range(BLOCKS)]
-        x_codes = [new_tile([P, M_OUT], U32, f"x_codes{b}") for b in range(BLOCKS)]
-        x_planes = [new_tile([P, M_OUT], U8, f"x_planes{b}") for b in range(BLOCKS)]
+        def gpsimd_copy(dst, src):
+            nc.gpsimd.tensor_scalar(dst, src, 1.0, 0.0, MULT, ADD)
 
-        def activate(b, t):
-            nc.scalar.activation(act[b][:, t, :], source[b, t][:], SILU, bias=silu_bias[:])
-            nc.gpsimd.tensor_scalar(x_rows[b][:, t, :], act[b][:, t, :], gain_sb[:, b, t : t + 1], 0.0, MULT, ADD)
-
-        def quantise_x(b, copies):
-            x_grouped = new_tile([P, M_OUT, PACK], BF16, f"x_grouped{b}")
-            width = M_OUT // len(copies)
-            for n, copy in enumerate(copies):
-                cols = slice(n * width, (n + 1) * width)
-                copy(
-                    x_grouped[:, cols, :].rearrange("p (c i) t -> p c t i", i=4),
-                    x_rows[b][:, :, cols].rearrange("p t (c i) -> p c t i", i=4),
-                )
-            nc.vector.quantize_mx(
-                out=x_codes[b][:].bitcast(FP8X4),
-                scales=x_planes[b][:],
-                in_=x_grouped[:].rearrange("p c t -> p (c t)"),
+        def interleave_x(copy, dst, b, c0, width):
+            copy(
+                dst.rearrange("p (c i) t -> p c t i", i=4),
+                x_rows[b][:, :, c0 : c0 + width].rearrange("p t (c i) -> p c t i", i=4),
             )
 
-        for t in range(PACK):
-            activate(0, t)
-        quantise_x(0, [gpsimd_copy])
+        def quantise_x(b, grouped_x, c0, width):
+            nc.vector.quantize_mx(
+                out=x_codes[b][:, c0 : c0 + width].bitcast(FP8X4),
+                scales=x_planes[b][:, c0 : c0 + width],
+                in_=grouped_x.rearrange("p c t -> p (c t)"),
+            )
+
+        half = M_OUT // 2
+        x0_first = new_tile([P, half, PACK], BF16, "x0_first")
+        x0_second = new_tile([P, half, PACK], BF16, "x0_second", "source11")
+        interleave_x(gpsimd_copy, x0_first[:], 0, 0, half)
+        interleave_x(nc.vector.tensor_copy, x0_second[:], 0, half, half)
+        quantise_x(0, x0_first[:], 0, half)
+        quantise_x(0, x0_second[:], half, half)
+        act.append(new_tile([P, PACK, M_OUT], F32, "act1", "w2_planes"))
         for t in range(PACK):
             activate(1, t)
-        quantise_x(1, [nc.vector.tensor_copy, nc.scalar.copy])
-        for t in range(2):
-            pick_dest(1, t, new_tile([P, M_OUT], F32, f"dest1{t}", f"source1{t + 2}")[:])
-        last_picks = new_tile([P, 2, M_OUT], F32, "last_picks", "x_grouped1")
-        for t in range(2):
-            pick_dest(1, t + 2, last_picks[:, t, :])
+        x1_grouped = new_tile([P, M_OUT, PACK], BF16, "x1_grouped", "x0_first")
+        interleave_x(nc.vector.tensor_copy, x1_grouped[:, 0:half, :], 1, 0, half)
+        interleave_x(nc.scalar.copy, x1_grouped[:, half:M_OUT, :], 1, half, half)
+        quantise_x(1, x1_grouped[:], 0, M_OUT)
+        pick_dest(0, 2, new_tile([P, M_OUT], F32, "dest02", "source11")[:])
+        late_picks = new_tile([P, 2, M_OUT], F32, "late_picks", "x0_first")
+        pick_dest(0, 3, late_picks[:, 0, :])
+        pick_dest(1, 0, late_picks[:, 1, :])
 
         y_banks = [psum.tile([P, BANK], F32, name=f"y_bank{i}", tag=f"bank{i}") for i in range(BLOCKS * PACK)]
         for a in range(BLOCKS):
@@ -276,18 +286,40 @@ def tile_list_ringing_residual_layer_kernel(
                 )
 
         out_rows = out.rearrange("(b p t) m -> b t p m", p=P, t=PACK)
-        for b in range(BLOCKS):
-            result = new_tile([P, PACK, M_OUT], F32, f"result{b}", f"raw{2 * b}0")
-            for t in range(PACK):
-                parts = 2 if (b, t) == (BLOCKS - 1, PACK - 1) else 1
-                for n in range(parts):
-                    cols = slice(n * M_OUT // parts, (n + 1) * M_OUT // parts)
-                    nc.vector.scalar_tensor_tensor(
-                        result[:, t, cols],
-                        dest[b, t][:, cols],
-                        skip_sb[:, b, t : t + 1],
-                        y_banks[b * PACK + t][:, cols],
-                        MULT,
-                        ADD,
-                    )
-                    nc.sync.dma_start(out_rows[b, t][:, cols], result[:, t, cols])
+        result = [new_tile([P, PACK, M_OUT], F32, f"result{b}", f"raw0{b}") for b in range(BLOCKS)]
+        gpsimd_tiles = [(0, 1), (0, 2), (0, 3), (1, 0)]
+        y_sb = new_tile([P, len(gpsimd_tiles), M_OUT], F32, "y_sb", "raw20_0")
+        skipped = new_tile([P, len(gpsimd_tiles), M_OUT], F32, "skipped", "x_rows1")
+
+        def finish_gpsimd(b, t):
+            n = gpsimd_tiles.index((b, t))
+            nc.scalar.activation(skipped[:, n, :], dest[b, t], COPY, scale=skip_sb[:, b, t : t + 1])
+            nc.scalar.copy(y_sb[:, n, :], y_banks[b * PACK + t][:])
+            nc.gpsimd.tensor_tensor(result[b][:, t, :], skipped[:, n, :], y_sb[:, n, :], ADD)
+            nc.sync.dma_start(out_rows[b, t], result[b][:, t, :])
+
+        def finish_vector(b, t, parts):
+            for n in range(parts):
+                cols = slice(n * M_OUT // parts, (n + 1) * M_OUT // parts)
+                nc.vector.scalar_tensor_tensor(
+                    result[b][:, t, cols],
+                    dest[b, t][:, cols],
+                    skip_sb[:, b, t : t + 1],
+                    y_banks[b * PACK + t][:, cols],
+                    MULT,
+                    ADD,
+                )
+                nc.sync.dma_start(out_rows[b, t][:, cols], result[b][:, t, cols])
+
+        finish_gpsimd(0, 1)
+        finish_vector(0, 0, 1)
+        last_picks = new_tile([P, 2, M_OUT], F32, "last_picks", "w1_codes20")
+        for t in range(2):
+            pick_dest(1, t + 1, last_picks[:, t, :])
+        finish_gpsimd(0, 2)
+        finish_gpsimd(0, 3)
+        finish_vector(1, 1, 1)
+        pick_dest(1, 3, dest[1, 1])
+        finish_gpsimd(1, 0)
+        finish_vector(1, 2, 1)
+        finish_vector(1, 3, 2)

@@ -110,6 +110,9 @@ def tile_list_ringing_residual_layer_kernel(
             nc.vector.tensor_copy(words[:], tab[a][:].bitcast(U32).indirect(entries))
             picked[a, u] = words[:]
 
+        def gpsimd_copy(dst, src):
+            nc.gpsimd.tensor_scalar(dst, src, 1.0, 0.0, MULT, ADD)
+
         grouped = {}
         w1_codes = {}
         w1_planes = {}
@@ -124,35 +127,32 @@ def tile_list_ringing_residual_layer_kernel(
             grouped[a, b] = new_tile([P, PACK, P, PACK], BF16, f"grouped{a}{b}", tag)
             interleave(copy, grouped[a, b], raw[a, b][:], 0, P)
 
-        def quantise_w1(a, b, parts):
-            w1_codes[a, b] = new_tile([P, K_PASS], U32, f"w1_codes{a}{b}")
-            w1_planes[a, b] = new_tile([P, K_PASS], U8, f"w1_planes{a}{b}")
-            flat = grouped[a, b][:].rearrange("p t m j -> p (t m j)")
-            width = K_PASS // parts
-            for i in range(parts):
-                cols = slice(i * width, (i + 1) * width)
-                nc.vector.quantize_mx(
-                    out=w1_codes[a, b][:, cols].bitcast(FP8X4),
-                    scales=w1_planes[a, b][:, cols],
-                    in_=flat[:, PACK * i * width : PACK * (i + 1) * width],
-                )
+        def quantise_w1(a, b, first, words, tag=None):
+            count = words.shape[1]
+            codes = new_tile([P, count * P], U32, f"w1_codes{a}{b}{first}", tag)
+            planes = new_tile([P, count * P], U8, f"w1_planes{a}{b}{first}")
+            nc.vector.quantize_mx(
+                out=codes[:].bitcast(FP8X4), scales=planes[:], in_=words.rearrange("p t m j -> p (t m j)")
+            )
+            for n in range(count):
+                w1_codes[a, b, first + n] = codes[:, n * P : (n + 1) * P]
+                w1_planes[a, b, first + n] = planes[:, n * P : (n + 1) * P]
 
         banks = {}
 
-        def first_product(a, b, t):
+        def first_product(order, a, b, t):
             for u in range(2):
-                if a == 0:
+                if a == order[0]:
                     banks[b, t, u] = psum.tile([P, BANK], F32, name=f"h_bank{b}{t}{u}", tag=f"bank{2 * t + u}")
-                rows = slice(t * P, (t + 1) * P)
                 cols = slice(u * BANK, (u + 1) * BANK)
                 nc.tensor.matmul_mx(
                     out=banks[b, t, u][:],
-                    lhsT=w1_codes[a, b][:, rows].bitcast(FP8X4),
-                    lhsT_scale=w1_planes[a, b][:, rows],
+                    lhsT=w1_codes[a, b, t].bitcast(FP8X4),
+                    lhsT_scale=w1_planes[a, b, t],
                     rhs=picked[a, u].bitcast(FP8X4),
                     rhs_scale=picked_planes[4 * (a + 1) : P, cols],
-                    start=(a == 0),
-                    stop=(a == K_PASSES - 1),
+                    start=(a == order[0]),
+                    stop=(a == order[-1]),
                 )
 
         h = [new_tile([P, PACK, S], F32, "h0", "tab0")]
@@ -164,7 +164,7 @@ def tile_list_ringing_residual_layer_kernel(
                 nc.scalar.copy(h[b][:, t, u * BANK : (u + 1) * BANK], banks[b, t, u][:])
 
         def pick_source(b, t):
-            source[b, t] = new_tile([P, M_OUT], F32, f"source{b}{t}", {(0, 0): "grouped01", (0, 3): "tab1"}.get((b, t)))
+            source[b, t] = new_tile([P, M_OUT], F32, f"source{b}{t}", "tab1" if (b, t) == (0, PACK - 1) else None)
             nc.vector.tensor_copy(source[b, t][:], h[b][:, t, :].indirect(pos1_sb[:]))
 
         def pick_dest(b, t, picks):
@@ -174,14 +174,14 @@ def tile_list_ringing_residual_layer_kernel(
         pick_words(0)
         nc.vector.tensor_copy(picked_planes[:], tab_planes[:].indirect(offs_sb[:]))
         interleave_w1(nc.scalar.copy, 0, 0)
-        quantise_w1(0, 0, 1)
+        quantise_w1(0, 0, 0, grouped[0, 0][:])
         for t in range(PACK):
-            first_product(0, 0, t)
+            first_product((0, 1, 2), 0, 0, t)
         pick_words(1)
         interleave_w1(nc.scalar.copy, 1, 0)
-        quantise_w1(1, 0, 1)
+        quantise_w1(1, 0, 0, grouped[1, 0][:])
         for t in range(PACK):
-            first_product(1, 0, t)
+            first_product((0, 1, 2), 1, 0, t)
         w2_sorted_planes = new_tile([P, BLOCKS * H], U8, "w2_sorted_planes")
         nc.vector.tensor_copy(
             w2_sorted_planes[:].rearrange("p (g t m) -> p g t m", t=PACK, m=P),
@@ -192,25 +192,40 @@ def tile_list_ringing_residual_layer_kernel(
         grouped[2, 0] = new_tile([P, PACK, P, PACK], BF16, "grouped20")
         interleave(nc.scalar.copy, grouped[2, 0], raw20[0][:], 0, P // 2)
         interleave(nc.vector.tensor_copy, grouped[2, 0], raw20[1][:], P // 2, P // 2)
-        quantise_w1(2, 0, PACK)
+        quantise_w1(2, 0, 0, grouped[2, 0][:, 0:1])
+        quantise_w1(2, 0, 1, grouped[2, 0][:, 1:2])
+        quantise_w1(2, 0, 2, grouped[2, 0][:, 2:4])
         for t in range(PACK):
-            first_product(2, 0, t)
+            first_product((0, 1, 2), 2, 0, t)
             empty_banks(0, t)
-        interleave_w1(nc.vector.tensor_copy, 0, 1)
-        quantise_w1(0, 1, 1)
         for t in range(PACK):
             pick_source(0, t)
 
-        interleave_w1(nc.scalar.copy, 1, 1, "w1_codes20")
-        quantise_w1(1, 1, 1)
+        def interleave_pair(copy, dst, a, b, i):
+            copy(
+                dst.rearrange("p h m j -> p m j h"),
+                raw[a, b][:].rearrange("p j (m i h) -> p i m j h", i=2, h=2)[:, i],
+            )
+
+        grouped[0, 1] = new_tile([P, PACK, P, PACK], BF16, "grouped01")
+        for i in range(2):
+            interleave_pair(gpsimd_copy, grouped[0, 1][:, 2 * i : 2 * i + 2], 0, 1, i)
+        for i, tag in enumerate(["w1_codes202", "grouped11b"]):
+            pair = new_tile([P, 2, P, PACK], BF16, f"grouped11_{i}", tag)
+            interleave_pair(nc.scalar.copy, pair[:], 1, 1, i)
+            quantise_w1(1, 1, 2 * i, pair[:])
+        pick_dest(0, 0, new_tile([P, M_OUT], F32, "dest00", "w1_codes202")[:])
+        quantise_w1(0, 1, 0, grouped[0, 1][:], "grouped11b")
         interleave_w1(nc.scalar.copy, 2, 1)
-        quantise_w1(2, 1, 2)
+        quantise_w1(2, 1, 0, grouped[2, 1][:, 0:2], "grouped01")
+        quantise_w1(2, 1, 2, grouped[2, 1][:, 2:4])
+        order = (1, 0, 2)
         for t in range(PACK):
-            for a in range(K_PASSES):
-                first_product(a, 1, t)
+            for a in order:
+                first_product(order, a, 1, t)
         act = [new_tile([P, PACK, M_OUT], F32, "act0", "raw21")]
         x_rows = [new_tile([P, PACK, M_OUT], BF16, f"x_rows{b}") for b in range(BLOCKS)]
-        x_codes = [new_tile([P, M_OUT], U32, f"x_codes{b}", ["x_rows0", None][b]) for b in range(BLOCKS)]
+        x_codes = [new_tile([P, M_OUT], U32, f"x_codes{b}", ["source11", None][b]) for b in range(BLOCKS)]
         x_planes = [new_tile([P, M_OUT], U8, f"x_planes{b}") for b in range(BLOCKS)]
 
         def activate(b, t):
@@ -233,47 +248,37 @@ def tile_list_ringing_residual_layer_kernel(
             w2_codes[:].bitcast(U16).rearrange("p (g t m) -> p g t m", t=PACK, m=P),
             w2_raw[:].rearrange("p a c -> p (a c)").bitcast(U16).rearrange("p (g m t) -> p g t m", t=PACK, m=P),
         )
-        pick_dest(0, 0, new_tile([P, M_OUT], F32, "dest00", "w1_codes20")[:])
         pick_dest(0, 1, new_tile([P, M_OUT], F32, "dest01", "w2_raw")[:])
 
-        def gpsimd_copy(dst, src):
-            nc.gpsimd.tensor_scalar(dst, src, 1.0, 0.0, MULT, ADD)
-
-        def interleave_x(copy, dst, b, c0, width):
-            copy(
-                dst.rearrange("p (c i) t -> p c t i", i=4),
-                x_rows[b][:, :, c0 : c0 + width].rearrange("p t (c i) -> p c t i", i=4),
+        def quantise_x(b, scalar_cols):
+            x_grouped = new_tile([P, M_OUT, PACK], BF16, f"x_grouped{b}")
+            if scalar_cols:
+                nc.scalar.copy(
+                    x_grouped[:, 0:scalar_cols, :].rearrange("p (c i) t -> p c t i", i=4),
+                    x_rows[b][:, :, 0:scalar_cols].rearrange("p t (c i) -> p c t i", i=4),
+                )
+            gpsimd_copy(
+                x_grouped[:, scalar_cols:M_OUT, :], x_rows[b][:, :, scalar_cols:M_OUT].rearrange("p t c -> p c t")
             )
-
-        def quantise_x(b, grouped_x, c0, width):
             nc.vector.quantize_mx(
-                out=x_codes[b][:, c0 : c0 + width].bitcast(FP8X4),
-                scales=x_planes[b][:, c0 : c0 + width],
-                in_=grouped_x.rearrange("p c t -> p (c t)"),
+                out=x_codes[b][:].bitcast(FP8X4),
+                scales=x_planes[b][:],
+                in_=x_grouped[:].rearrange("p c t -> p (c t)"),
             )
 
-        half = M_OUT // 2
-        x0_first = new_tile([P, half, PACK], BF16, "x0_first")
-        x0_second = new_tile([P, half, PACK], BF16, "x0_second", "source11")
-        interleave_x(gpsimd_copy, x0_first[:], 0, 0, half)
-        interleave_x(nc.vector.tensor_copy, x0_second[:], 0, half, half)
-        quantise_x(0, x0_first[:], 0, half)
-        quantise_x(0, x0_second[:], half, half)
+        quantise_x(0, 0)
         act.append(new_tile([P, PACK, M_OUT], F32, "act1", "w2_planes"))
         for t in range(PACK):
             activate(1, t)
-        x1_grouped = new_tile([P, M_OUT, PACK], BF16, "x1_grouped", "x0_first")
-        interleave_x(nc.vector.tensor_copy, x1_grouped[:, 0:half, :], 1, 0, half)
-        interleave_x(nc.scalar.copy, x1_grouped[:, half:M_OUT, :], 1, half, half)
-        quantise_x(1, x1_grouped[:], 0, M_OUT)
-        pick_dest(0, 2, new_tile([P, M_OUT], F32, "dest02", "source11")[:])
-        late_picks = new_tile([P, 2, M_OUT], F32, "late_picks", "x0_first")
-        pick_dest(0, 3, late_picks[:, 0, :])
-        pick_dest(1, 0, late_picks[:, 1, :])
+        quantise_x(1, 320)
+        middle_picks = new_tile([P, 3, M_OUT], F32, "middle_picks", "x_grouped0")
+        for n, (b, t) in enumerate([(0, 2), (0, 3), (1, 0)]):
+            pick_dest(b, t, middle_picks[:, n, :])
+        pick_dest(1, 1, new_tile([P, M_OUT], F32, "dest11", "x_grouped1")[:])
 
         y_banks = [psum.tile([P, BANK], F32, name=f"y_bank{i}", tag=f"bank{i}") for i in range(BLOCKS * PACK)]
         for a in range(BLOCKS):
-            for i in range(BLOCKS * PACK):
+            for i in (0, 4, 1, 5, 2, 6, 3, 7):
                 c0 = a * H + i * P
                 nc.tensor.matmul_mx(
                     out=y_banks[i][:],
@@ -287,7 +292,7 @@ def tile_list_ringing_residual_layer_kernel(
 
         out_rows = out.rearrange("(b p t) m -> b t p m", p=P, t=PACK)
         result = [new_tile([P, PACK, M_OUT], F32, f"result{b}", f"raw0{b}") for b in range(BLOCKS)]
-        gpsimd_tiles = [(0, 1), (0, 2), (0, 3), (1, 0)]
+        gpsimd_tiles = [(0, 0), (0, 1), (0, 2), (0, 3)]
         y_sb = new_tile([P, len(gpsimd_tiles), M_OUT], F32, "y_sb", "raw20_0")
         skipped = new_tile([P, len(gpsimd_tiles), M_OUT], F32, "skipped", "x_rows1")
 
@@ -311,15 +316,13 @@ def tile_list_ringing_residual_layer_kernel(
                 )
                 nc.sync.dma_start(out_rows[b, t][:, cols], result[b][:, t, cols])
 
+        finish_gpsimd(0, 0)
+        finish_vector(1, 0, 1)
+        pick_dest(1, 2, dest[1, 0])
         finish_gpsimd(0, 1)
-        finish_vector(0, 0, 1)
-        last_picks = new_tile([P, 2, M_OUT], F32, "last_picks", "w1_codes20")
-        for t in range(2):
-            pick_dest(1, t + 1, last_picks[:, t, :])
         finish_gpsimd(0, 2)
-        finish_gpsimd(0, 3)
         finish_vector(1, 1, 1)
         pick_dest(1, 3, dest[1, 1])
-        finish_gpsimd(1, 0)
+        finish_gpsimd(0, 3)
         finish_vector(1, 2, 1)
         finish_vector(1, 3, 2)

@@ -24,6 +24,7 @@ K_PASS = P * PACK
 BANK = 512
 K_PASSES = K // K_PASS
 BLOCKS = H // K_PASS
+GPSIMD_SHARE = 64
 
 
 def tile_list_ringing_residual_layer_kernel(
@@ -83,6 +84,8 @@ def tile_list_ringing_residual_layer_kernel(
         for n in range(2):
             rows = w1[2 * K_PASS : 3 * K_PASS, n * half : (n + 1) * half]
             nc.sync.dma_start(raw20[n][:], rows.rearrange("(p j) c -> p j c", j=PACK))
+        w2_raw = new_tile([P, BLOCKS, H // 2], I32, "w2_raw", "tab0")
+        nc.sync.dma_start(w2_raw[:], w2_words.bitcast(I32).rearrange("a p c -> p a c"))
         nc.sync.dma_start(pos1_sb[:], pos1)
         load_w1(0, 1)
         nc.sync.dma_start(pos2_sb[:], pos2)
@@ -92,8 +95,6 @@ def tile_list_ringing_residual_layer_kernel(
         load_w1(2, 1)
         skip_sb = new_tile([P, BLOCKS, PACK], F32, "skip_sb")
         nc.sync.dma_start(skip_sb[:], skip.rearrange("(b p t) -> p b t", p=P, t=PACK))
-        w2_raw = new_tile([P, BLOCKS, H // 2], I32, "w2_raw")
-        nc.sync.dma_start(w2_raw[:], w2_words.bitcast(I32).rearrange("a p c -> p a c"))
 
         picked = {}
         picked_planes = new_tile([P, S], U8, "picked_planes")
@@ -155,13 +156,14 @@ def tile_list_ringing_residual_layer_kernel(
                     stop=(a == order[-1]),
                 )
 
-        h = [new_tile([P, PACK, S], F32, "h0", "tab0")]
+        h = []
         source = {}
         dest = {}
 
         def empty_banks(b, t):
             for u in range(2):
-                nc.scalar.copy(h[b][:, t, u * BANK : (u + 1) * BANK], banks[b, t, u][:])
+                copy = nc.vector.tensor_copy if (b, t, u) == (0, 0, 1) else nc.scalar.copy
+                copy(h[b][:, t, u * BANK : (u + 1) * BANK], banks[b, t, u][:])
 
         def pick_source(b, t):
             source[b, t] = new_tile([P, M_OUT], F32, f"source{b}{t}", "tab1" if (b, t) == (0, PACK - 1) else None)
@@ -191,29 +193,36 @@ def tile_list_ringing_residual_layer_kernel(
         pick_words_half(2, 1, "w2_planes")
         grouped[2, 0] = new_tile([P, PACK, P, PACK], BF16, "grouped20")
         interleave(nc.scalar.copy, grouped[2, 0], raw20[0][:], 0, P // 2)
-        interleave(nc.vector.tensor_copy, grouped[2, 0], raw20[1][:], P // 2, P // 2)
+        interleave(nc.vector.tensor_copy, grouped[2, 0], raw20[1][:, :, 0 : PACK * 40], P // 2, 40)
+        interleave(nc.scalar.copy, grouped[2, 0], raw20[1][:, :, PACK * 40 : PACK * 64], P // 2 + 40, 24)
         quantise_w1(2, 0, 0, grouped[2, 0][:, 0:1])
         quantise_w1(2, 0, 1, grouped[2, 0][:, 1:2])
         quantise_w1(2, 0, 2, grouped[2, 0][:, 2:4])
+        w2_codes = new_tile([P, BLOCKS * 2 * H], U8, "w2_codes")
+        nc.vector.tensor_copy(
+            w2_codes[:].bitcast(U16).rearrange("p (g t m) -> p g t m", t=PACK, m=P),
+            w2_raw[:].rearrange("p a c -> p (a c)").bitcast(U16).rearrange("p (g m t) -> p g t m", t=PACK, m=P),
+        )
+        h.append(new_tile([P, PACK, S], F32, "h0", "tab0"))
         for t in range(PACK):
             first_product((0, 1, 2), 2, 0, t)
             empty_banks(0, t)
         for t in range(PACK):
             pick_source(0, t)
 
-        def interleave_pair(copy, dst, a, b, i):
-            copy(
-                dst.rearrange("p h m j -> p m j h"),
-                raw[a, b][:].rearrange("p j (m i h) -> p i m j h", i=2, h=2)[:, i],
-            )
+        def interleave_pair(copy, dst, src, i):
+            copy(dst.rearrange("p h m j -> p m j h"), src.rearrange("p j (m i h) -> p i m j h", i=2, h=2)[:, i])
 
         grouped[0, 1] = new_tile([P, PACK, P, PACK], BF16, "grouped01")
         for i in range(2):
-            interleave_pair(gpsimd_copy, grouped[0, 1][:, 2 * i : 2 * i + 2], 0, 1, i)
+            share = grouped[0, 1][:, 2 * i : 2 * i + 2, 0:GPSIMD_SHARE]
+            interleave_pair(gpsimd_copy, share, raw[0, 1][:, :, 0 : PACK * GPSIMD_SHARE], i)
         for i, tag in enumerate(["w1_codes202", "grouped11b"]):
             pair = new_tile([P, 2, P, PACK], BF16, f"grouped11_{i}", tag)
-            interleave_pair(nc.scalar.copy, pair[:], 1, 1, i)
+            interleave_pair(nc.scalar.copy, pair[:], raw[1, 1][:], i)
             quantise_w1(1, 1, 2 * i, pair[:])
+        rest = raw[0, 1][:, :, PACK * GPSIMD_SHARE : K_PASS]
+        interleave(nc.scalar.copy, grouped[0, 1], rest, GPSIMD_SHARE, P - GPSIMD_SHARE)
         pick_dest(0, 0, new_tile([P, M_OUT], F32, "dest00", "w1_codes202")[:])
         quantise_w1(0, 1, 0, grouped[0, 1][:], "grouped11b")
         interleave_w1(nc.scalar.copy, 2, 1)
@@ -243,12 +252,9 @@ def tile_list_ringing_residual_layer_kernel(
             empty_banks(1, t)
             pick_source(1, t)
 
-        w2_codes = new_tile([P, BLOCKS * 2 * H], U8, "w2_codes", "grouped21")
-        nc.vector.tensor_copy(
-            w2_codes[:].bitcast(U16).rearrange("p (g t m) -> p g t m", t=PACK, m=P),
-            w2_raw[:].rearrange("p a c -> p (a c)").bitcast(U16).rearrange("p (g m t) -> p g t m", t=PACK, m=P),
-        )
-        pick_dest(0, 1, new_tile([P, M_OUT], F32, "dest01", "w2_raw")[:])
+        early_picks = new_tile([P, 2, M_OUT], F32, "early_picks", "grouped21")
+        for t in range(2):
+            pick_dest(0, t + 1, early_picks[:, t, :])
 
         def quantise_x(b, scalar_cols):
             x_grouped = new_tile([P, M_OUT, PACK], BF16, f"x_grouped{b}")
@@ -272,13 +278,13 @@ def tile_list_ringing_residual_layer_kernel(
             activate(1, t)
         quantise_x(1, 320)
         middle_picks = new_tile([P, 3, M_OUT], F32, "middle_picks", "x_grouped0")
-        for n, (b, t) in enumerate([(0, 2), (0, 3), (1, 0)]):
+        for n, (b, t) in enumerate([(0, 3), (1, 0), (1, 1)]):
             pick_dest(b, t, middle_picks[:, n, :])
-        pick_dest(1, 1, new_tile([P, M_OUT], F32, "dest11", "x_grouped1")[:])
+        pick_dest(1, 2, new_tile([P, M_OUT], F32, "dest12", "x_grouped1")[:])
 
         y_banks = [psum.tile([P, BANK], F32, name=f"y_bank{i}", tag=f"bank{i}") for i in range(BLOCKS * PACK)]
         for a in range(BLOCKS):
-            for i in (0, 4, 1, 5, 2, 6, 3, 7):
+            for i in (0, 3, 1, 4, 2, 5, 6, 7):
                 c0 = a * H + i * P
                 nc.tensor.matmul_mx(
                     out=y_banks[i][:],
@@ -292,7 +298,7 @@ def tile_list_ringing_residual_layer_kernel(
 
         out_rows = out.rearrange("(b p t) m -> b t p m", p=P, t=PACK)
         result = [new_tile([P, PACK, M_OUT], F32, f"result{b}", f"raw0{b}") for b in range(BLOCKS)]
-        gpsimd_tiles = [(0, 0), (0, 1), (0, 2), (0, 3)]
+        gpsimd_tiles = [(0, 0), (0, 1), (0, 2)]
         y_sb = new_tile([P, len(gpsimd_tiles), M_OUT], F32, "y_sb", "raw20_0")
         skipped = new_tile([P, len(gpsimd_tiles), M_OUT], F32, "skipped", "x_rows1")
 
@@ -316,13 +322,12 @@ def tile_list_ringing_residual_layer_kernel(
                 )
                 nc.sync.dma_start(out_rows[b, t][:, cols], result[b][:, t, cols])
 
+        finish_vector(0, 3, 1)
         finish_gpsimd(0, 0)
         finish_vector(1, 0, 1)
-        pick_dest(1, 2, dest[1, 0])
+        pick_dest(1, 3, dest[1, 0])
         finish_gpsimd(0, 1)
-        finish_gpsimd(0, 2)
         finish_vector(1, 1, 1)
-        pick_dest(1, 3, dest[1, 1])
-        finish_gpsimd(0, 3)
+        finish_gpsimd(0, 2)
         finish_vector(1, 2, 1)
         finish_vector(1, 3, 2)

@@ -24,7 +24,6 @@ K_PASS = P * PACK
 BANK = 512
 K_PASSES = K // K_PASS
 BLOCKS = H // K_PASS
-GPSIMD_SHARE = 64
 
 
 def tile_list_ringing_residual_layer_kernel(
@@ -67,14 +66,14 @@ def tile_list_ringing_residual_layer_kernel(
         load_tab(0)
         load_w1(0, 0)
         for q in range(4):
-            nc.sync.dma_start(
+            nc.gpsimd.dma_start(
                 tab_planes[32 * q + 4 : 32 * q + 4 + 4 * K_PASSES, :].bitcast(I32),
                 tab_scales[:, 4 * q : 4 * q + 4, :].bitcast(I32),
             )
         load_tab(1)
         load_w1(1, 0)
         for q in range(4):
-            nc.sync.dma_start(
+            nc.gpsimd.dma_start(
                 w2_planes[32 * q : 32 * q + 4, :].bitcast(I32).rearrange("r (a c) -> r a c", a=BLOCKS),
                 w2_scales[:, 4 * q : 4 * q + 4, :].bitcast(I32).rearrange("a r c -> r a c"),
             )
@@ -91,10 +90,10 @@ def tile_list_ringing_residual_layer_kernel(
         nc.sync.dma_start(pos2_sb[:], pos2)
         load_w1(1, 1)
         gain_sb = new_tile([P, BLOCKS, PACK], F32, "gain_sb")
-        nc.sync.dma_start(gain_sb[:], gain.rearrange("(b p t) -> p b t", p=P, t=PACK))
+        nc.gpsimd.dma_start(gain_sb[:], gain.rearrange("(b p t) -> p b t", p=P, t=PACK))
         load_w1(2, 1)
         skip_sb = new_tile([P, BLOCKS, PACK], F32, "skip_sb")
-        nc.sync.dma_start(skip_sb[:], skip.rearrange("(b p t) -> p b t", p=P, t=PACK))
+        nc.gpsimd.dma_start(skip_sb[:], skip.rearrange("(b p t) -> p b t", p=P, t=PACK))
 
         picked = {}
         picked_planes = new_tile([P, S], U8, "picked_planes")
@@ -128,9 +127,9 @@ def tile_list_ringing_residual_layer_kernel(
             grouped[a, b] = new_tile([P, PACK, P, PACK], BF16, f"grouped{a}{b}", tag)
             interleave(copy, grouped[a, b], raw[a, b][:], 0, P)
 
-        def quantise_w1(a, b, first, words, tag=None):
+        def quantise_w1(a, b, first, words):
             count = words.shape[1]
-            codes = new_tile([P, count * P], U32, f"w1_codes{a}{b}{first}", tag)
+            codes = new_tile([P, count * P], U32, f"w1_codes{a}{b}{first}")
             planes = new_tile([P, count * P], U8, f"w1_planes{a}{b}{first}")
             nc.vector.quantize_mx(
                 out=codes[:].bitcast(FP8X4), scales=planes[:], in_=words.rearrange("p t m j -> p (t m j)")
@@ -141,9 +140,9 @@ def tile_list_ringing_residual_layer_kernel(
 
         banks = {}
 
-        def first_product(order, a, b, t):
+        def first_product(a, b, t):
             for u in range(2):
-                if a == order[0]:
+                if a == 0:
                     banks[b, t, u] = psum.tile([P, BANK], F32, name=f"h_bank{b}{t}{u}", tag=f"bank{2 * t + u}")
                 cols = slice(u * BANK, (u + 1) * BANK)
                 nc.tensor.matmul_mx(
@@ -152,8 +151,8 @@ def tile_list_ringing_residual_layer_kernel(
                     lhsT_scale=w1_planes[a, b, t],
                     rhs=picked[a, u].bitcast(FP8X4),
                     rhs_scale=picked_planes[4 * (a + 1) : P, cols],
-                    start=(a == order[0]),
-                    stop=(a == order[-1]),
+                    start=(a == 0),
+                    stop=(a == K_PASSES - 1),
                 )
 
         h = []
@@ -166,7 +165,7 @@ def tile_list_ringing_residual_layer_kernel(
                 copy(h[b][:, t, u * BANK : (u + 1) * BANK], banks[b, t, u][:])
 
         def pick_source(b, t):
-            source[b, t] = new_tile([P, M_OUT], F32, f"source{b}{t}", "tab1" if (b, t) == (0, PACK - 1) else None)
+            source[b, t] = new_tile([P, M_OUT], F32, f"source{b}{t}", {(0, 0): "grouped01", (0, 2): "w1_codes202", (0, 3): "tab1"}.get((b, t)))
             nc.vector.tensor_copy(source[b, t][:], h[b][:, t, :].indirect(pos1_sb[:]))
 
         def pick_dest(b, t, picks):
@@ -178,12 +177,12 @@ def tile_list_ringing_residual_layer_kernel(
         interleave_w1(nc.scalar.copy, 0, 0)
         quantise_w1(0, 0, 0, grouped[0, 0][:])
         for t in range(PACK):
-            first_product((0, 1, 2), 0, 0, t)
+            first_product(0, 0, t)
         pick_words(1)
         interleave_w1(nc.scalar.copy, 1, 0)
         quantise_w1(1, 0, 0, grouped[1, 0][:])
         for t in range(PACK):
-            first_product((0, 1, 2), 1, 0, t)
+            first_product(1, 0, t)
         w2_sorted_planes = new_tile([P, BLOCKS * H], U8, "w2_sorted_planes")
         nc.vector.tensor_copy(
             w2_sorted_planes[:].rearrange("p (g t m) -> p g t m", t=PACK, m=P),
@@ -205,33 +204,22 @@ def tile_list_ringing_residual_layer_kernel(
         )
         h.append(new_tile([P, PACK, S], F32, "h0", "tab0"))
         for t in range(PACK):
-            first_product((0, 1, 2), 2, 0, t)
+            first_product(2, 0, t)
             empty_banks(0, t)
-        for t in range(PACK):
+        interleave_w1(nc.vector.tensor_copy, 0, 1)
+        quantise_w1(0, 1, 0, grouped[0, 1][:])
+        for t in range(2):
             pick_source(0, t)
-
-        def interleave_pair(copy, dst, src, i):
-            copy(dst.rearrange("p h m j -> p m j h"), src.rearrange("p j (m i h) -> p i m j h", i=2, h=2)[:, i])
-
-        grouped[0, 1] = new_tile([P, PACK, P, PACK], BF16, "grouped01")
-        for i in range(2):
-            share = grouped[0, 1][:, 2 * i : 2 * i + 2, 0:GPSIMD_SHARE]
-            interleave_pair(gpsimd_copy, share, raw[0, 1][:, :, 0 : PACK * GPSIMD_SHARE], i)
-        for i, tag in enumerate(["w1_codes202", "grouped11b"]):
-            pair = new_tile([P, 2, P, PACK], BF16, f"grouped11_{i}", tag)
-            interleave_pair(nc.scalar.copy, pair[:], raw[1, 1][:], i)
-            quantise_w1(1, 1, 2 * i, pair[:])
-        rest = raw[0, 1][:, :, PACK * GPSIMD_SHARE : K_PASS]
-        interleave(nc.scalar.copy, grouped[0, 1], rest, GPSIMD_SHARE, P - GPSIMD_SHARE)
-        pick_dest(0, 0, new_tile([P, M_OUT], F32, "dest00", "w1_codes202")[:])
-        quantise_w1(0, 1, 0, grouped[0, 1][:], "grouped11b")
+        interleave_w1(nc.scalar.copy, 1, 1, "w1_codes202")
+        quantise_w1(1, 1, 0, grouped[1, 1][:])
+        for t in range(2, PACK):
+            pick_source(0, t)
         interleave_w1(nc.scalar.copy, 2, 1)
-        quantise_w1(2, 1, 0, grouped[2, 1][:, 0:2], "grouped01")
+        quantise_w1(2, 1, 0, grouped[2, 1][:, 0:2])
         quantise_w1(2, 1, 2, grouped[2, 1][:, 2:4])
-        order = (1, 0, 2)
         for t in range(PACK):
-            for a in order:
-                first_product(order, a, 1, t)
+            for a in range(K_PASSES):
+                first_product(a, 1, t)
         act = [new_tile([P, PACK, M_OUT], F32, "act0", "raw21")]
         x_rows = [new_tile([P, PACK, M_OUT], BF16, f"x_rows{b}") for b in range(BLOCKS)]
         x_codes = [new_tile([P, M_OUT], U32, f"x_codes{b}", ["source11", None][b]) for b in range(BLOCKS)]
@@ -254,7 +242,7 @@ def tile_list_ringing_residual_layer_kernel(
 
         early_picks = new_tile([P, 2, M_OUT], F32, "early_picks", "grouped21")
         for t in range(2):
-            pick_dest(0, t + 1, early_picks[:, t, :])
+            pick_dest(0, t, early_picks[:, t, :])
 
         def quantise_x(b, scalar_cols):
             x_grouped = new_tile([P, M_OUT, PACK], BF16, f"x_grouped{b}")
@@ -278,9 +266,9 @@ def tile_list_ringing_residual_layer_kernel(
             activate(1, t)
         quantise_x(1, 320)
         middle_picks = new_tile([P, 3, M_OUT], F32, "middle_picks", "x_grouped0")
-        for n, (b, t) in enumerate([(0, 3), (1, 0), (1, 1)]):
+        for n, (b, t) in enumerate([(0, 2), (0, 3), (1, 0)]):
             pick_dest(b, t, middle_picks[:, n, :])
-        pick_dest(1, 2, new_tile([P, M_OUT], F32, "dest12", "x_grouped1")[:])
+        pick_dest(1, 1, new_tile([P, M_OUT], F32, "dest11", "x_grouped1")[:])
 
         y_banks = [psum.tile([P, BANK], F32, name=f"y_bank{i}", tag=f"bank{i}") for i in range(BLOCKS * PACK)]
         for a in range(BLOCKS):
@@ -300,13 +288,17 @@ def tile_list_ringing_residual_layer_kernel(
         result = [new_tile([P, PACK, M_OUT], F32, f"result{b}", f"raw0{b}") for b in range(BLOCKS)]
         gpsimd_tiles = [(0, 0), (0, 1), (0, 2)]
         y_sb = new_tile([P, len(gpsimd_tiles), M_OUT], F32, "y_sb", "raw20_0")
-        skipped = new_tile([P, len(gpsimd_tiles), M_OUT], F32, "skipped", "x_rows1")
+        skipped = [new_tile([P, 2, M_OUT], F32, f"skipped{b}", f"x_rows{b}") for b in range(BLOCKS)]
 
         def finish_gpsimd(b, t):
             n = gpsimd_tiles.index((b, t))
-            nc.scalar.activation(skipped[:, n, :], dest[b, t], COPY, scale=skip_sb[:, b, t : t + 1])
+            term = skipped[n // 2][:, n % 2, :]
+            if n < 2:
+                nc.gpsimd.tensor_scalar(term, dest[b, t], skip_sb[:, b, t : t + 1], 0.0, MULT, ADD)
+            else:
+                nc.scalar.activation(term, dest[b, t], COPY, scale=skip_sb[:, b, t : t + 1])
             nc.scalar.copy(y_sb[:, n, :], y_banks[b * PACK + t][:])
-            nc.gpsimd.tensor_tensor(result[b][:, t, :], skipped[:, n, :], y_sb[:, n, :], ADD)
+            nc.gpsimd.tensor_tensor(result[b][:, t, :], term, y_sb[:, n, :], ADD)
             nc.sync.dma_start(out_rows[b, t], result[b][:, t, :])
 
         def finish_vector(b, t, parts):
@@ -325,9 +317,10 @@ def tile_list_ringing_residual_layer_kernel(
         finish_vector(0, 3, 1)
         finish_gpsimd(0, 0)
         finish_vector(1, 0, 1)
-        pick_dest(1, 3, dest[1, 0])
+        pick_dest(1, 2, dest[1, 0])
         finish_gpsimd(0, 1)
         finish_vector(1, 1, 1)
+        pick_dest(1, 3, dest[1, 1])
         finish_gpsimd(0, 2)
         finish_vector(1, 2, 1)
         finish_vector(1, 3, 2)

@@ -62,8 +62,8 @@ def tile_list_ringing_residual_layer_kernel(
             rows = w1[a * K_PASS : (a + 1) * K_PASS, b * K_PASS : (b + 1) * K_PASS]
             nc.sync.dma_start(raw[a, b][:], rows.rearrange("(p j) c -> p j c", j=PACK))
 
-        nc.sync.dma_start(offs_sb[:], offs)
         load_tab(0)
+        nc.sync.dma_start(offs_sb[:], offs)
         load_w1(0, 0)
         for q in range(4):
             nc.gpsimd.dma_start(
@@ -83,8 +83,6 @@ def tile_list_ringing_residual_layer_kernel(
         for n in range(2):
             rows = w1[2 * K_PASS : 3 * K_PASS, n * half : (n + 1) * half]
             nc.sync.dma_start(raw20[n][:], rows.rearrange("(p j) c -> p j c", j=PACK))
-        w2_raw = new_tile([P, BLOCKS, H // 2], I32, "w2_raw", "tab0")
-        nc.sync.dma_start(w2_raw[:], w2_words.bitcast(I32).rearrange("a p c -> p a c"))
         nc.sync.dma_start(pos1_sb[:], pos1)
         load_w1(0, 1)
         nc.sync.dma_start(pos2_sb[:], pos2)
@@ -94,6 +92,8 @@ def tile_list_ringing_residual_layer_kernel(
         load_w1(2, 1)
         skip_sb = new_tile([P, BLOCKS, PACK], F32, "skip_sb")
         nc.gpsimd.dma_start(skip_sb[:], skip.rearrange("(b p t) -> p b t", p=P, t=PACK))
+        w2_raw = new_tile([P, BLOCKS, H // 2], I32, "w2_raw")
+        nc.sync.dma_start(w2_raw[:], w2_words.bitcast(I32).rearrange("a p c -> p a c"))
 
         picked = {}
         picked_planes = new_tile([P, S], U8, "picked_planes")
@@ -123,8 +123,8 @@ def tile_list_ringing_residual_layer_kernel(
                 src.rearrange("p j (m i h) -> p i m j h", i=2, h=2),
             )
 
-        def interleave_w1(copy, a, b, tag=None):
-            grouped[a, b] = new_tile([P, PACK, P, PACK], BF16, f"grouped{a}{b}", tag)
+        def interleave_w1(copy, a, b):
+            grouped[a, b] = new_tile([P, PACK, P, PACK], BF16, f"grouped{a}{b}")
             interleave(copy, grouped[a, b], raw[a, b][:], 0, P)
 
         def quantise_w1(a, b, first, words):
@@ -161,19 +161,18 @@ def tile_list_ringing_residual_layer_kernel(
 
         def empty_banks(b, t):
             for u in range(2):
-                copy = nc.vector.tensor_copy if (b, t, u) == (0, 0, 1) else nc.scalar.copy
-                copy(h[b][:, t, u * BANK : (u + 1) * BANK], banks[b, t, u][:])
+                nc.scalar.copy(h[b][:, t, u * BANK : (u + 1) * BANK], banks[b, t, u][:])
 
         def pick_source(b, t):
-            source[b, t] = new_tile([P, M_OUT], F32, f"source{b}{t}", {(0, 0): "grouped01", (0, 2): "w1_codes202", (0, 3): "tab1"}.get((b, t)))
+            source[b, t] = new_tile([P, M_OUT], F32, f"source{b}{t}", {(0, 0): "raw01", (0, 2): "w1_codes202", (0, 3): "tab1"}.get((b, t)))
             nc.vector.tensor_copy(source[b, t][:], h[b][:, t, :].indirect(pos1_sb[:]))
 
         def pick_dest(b, t, picks):
             dest[b, t] = picks
             nc.vector.tensor_copy(picks, h[b][:, t, :].indirect(pos2_sb[:]))
 
-        pick_words(0)
         nc.vector.tensor_copy(picked_planes[:], tab_planes[:].indirect(offs_sb[:]))
+        pick_words(0)
         interleave_w1(nc.scalar.copy, 0, 0)
         quantise_w1(0, 0, 0, grouped[0, 0][:])
         for t in range(PACK):
@@ -197,11 +196,6 @@ def tile_list_ringing_residual_layer_kernel(
         quantise_w1(2, 0, 0, grouped[2, 0][:, 0:1])
         quantise_w1(2, 0, 1, grouped[2, 0][:, 1:2])
         quantise_w1(2, 0, 2, grouped[2, 0][:, 2:4])
-        w2_codes = new_tile([P, BLOCKS * 2 * H], U8, "w2_codes")
-        nc.vector.tensor_copy(
-            w2_codes[:].bitcast(U16).rearrange("p (g t m) -> p g t m", t=PACK, m=P),
-            w2_raw[:].rearrange("p a c -> p (a c)").bitcast(U16).rearrange("p (g m t) -> p g t m", t=PACK, m=P),
-        )
         h.append(new_tile([P, PACK, S], F32, "h0", "tab0"))
         for t in range(PACK):
             first_product(2, 0, t)
@@ -210,19 +204,26 @@ def tile_list_ringing_residual_layer_kernel(
         quantise_w1(0, 1, 0, grouped[0, 1][:])
         for t in range(2):
             pick_source(0, t)
-        interleave_w1(nc.scalar.copy, 1, 1, "w1_codes202")
-        quantise_w1(1, 1, 0, grouped[1, 1][:])
+
+        def prepare_in_pairs(a, b, tags):
+            for i, tag in enumerate(tags):
+                pair = new_tile([P, 2, P, PACK], BF16, f"pair{a}{b}{i}", tag)
+                nc.scalar.copy(
+                    pair[:].rearrange("p h m j -> p m j h"),
+                    raw[a, b][:].rearrange("p j (m i h) -> p i m j h", i=2, h=2)[:, i],
+                )
+                quantise_w1(a, b, 2 * i, pair[:])
+
+        prepare_in_pairs(1, 1, ["w1_codes202", "w1_planes202"])
         for t in range(2, PACK):
             pick_source(0, t)
-        interleave_w1(nc.scalar.copy, 2, 1)
-        quantise_w1(2, 1, 0, grouped[2, 1][:, 0:2])
-        quantise_w1(2, 1, 2, grouped[2, 1][:, 2:4])
+        prepare_in_pairs(2, 1, ["w1_codes200", "w1_codes201"])
         for t in range(PACK):
             for a in range(K_PASSES):
                 first_product(a, 1, t)
         act = [new_tile([P, PACK, M_OUT], F32, "act0", "raw21")]
         x_rows = [new_tile([P, PACK, M_OUT], BF16, f"x_rows{b}") for b in range(BLOCKS)]
-        x_codes = [new_tile([P, M_OUT], U32, f"x_codes{b}", ["source11", None][b]) for b in range(BLOCKS)]
+        x_codes = [new_tile([P, M_OUT], U32, f"x_codes{b}", ["source10", None][b]) for b in range(BLOCKS)]
         x_planes = [new_tile([P, M_OUT], U8, f"x_planes{b}") for b in range(BLOCKS)]
 
         def activate(b, t):
@@ -240,9 +241,12 @@ def tile_list_ringing_residual_layer_kernel(
             empty_banks(1, t)
             pick_source(1, t)
 
-        early_picks = new_tile([P, 2, M_OUT], F32, "early_picks", "grouped21")
-        for t in range(2):
-            pick_dest(0, t, early_picks[:, t, :])
+        w2_codes = new_tile([P, BLOCKS * 2 * H], U8, "w2_codes", "w1_codes200")
+        nc.vector.tensor_copy(
+            w2_codes[:].bitcast(U16).rearrange("p (g t m) -> p g t m", t=PACK, m=P),
+            w2_raw[:].rearrange("p a c -> p (a c)").bitcast(U16).rearrange("p (g m t) -> p g t m", t=PACK, m=P),
+        )
+        pick_dest(0, 0, new_tile([P, M_OUT], F32, "dest00", "w1_codes201")[:])
 
         def quantise_x(b, scalar_cols):
             x_grouped = new_tile([P, M_OUT, PACK], BF16, f"x_grouped{b}")
@@ -265,14 +269,16 @@ def tile_list_ringing_residual_layer_kernel(
         for t in range(PACK):
             activate(1, t)
         quantise_x(1, 320)
-        middle_picks = new_tile([P, 3, M_OUT], F32, "middle_picks", "x_grouped0")
-        for n, (b, t) in enumerate([(0, 2), (0, 3), (1, 0)]):
+        middle_picks = new_tile([P, 3, M_OUT], F32, "middle_picks", "source11")
+        for n, (b, t) in enumerate([(0, 1), (0, 2), (0, 3)]):
             pick_dest(b, t, middle_picks[:, n, :])
-        pick_dest(1, 1, new_tile([P, M_OUT], F32, "dest11", "x_grouped1")[:])
+        late_picks = new_tile([P, 3, M_OUT], F32, "late_picks", "x_rows1")
+        for t in range(3):
+            pick_dest(1, t, late_picks[:, t, :])
 
         y_banks = [psum.tile([P, BANK], F32, name=f"y_bank{i}", tag=f"bank{i}") for i in range(BLOCKS * PACK)]
         for a in range(BLOCKS):
-            for i in (0, 3, 1, 4, 2, 5, 6, 7):
+            for i in range(BLOCKS * PACK):
                 c0 = a * H + i * P
                 nc.tensor.matmul_mx(
                     out=y_banks[i][:],
@@ -285,21 +291,21 @@ def tile_list_ringing_residual_layer_kernel(
                 )
 
         out_rows = out.rearrange("(b p t) m -> b t p m", p=P, t=PACK)
-        result = [new_tile([P, PACK, M_OUT], F32, f"result{b}", f"raw0{b}") for b in range(BLOCKS)]
-        gpsimd_tiles = [(0, 0), (0, 1), (0, 2)]
+        result = [new_tile([P, PACK, M_OUT], F32, f"result{b}", f"raw{b}0") for b in range(BLOCKS)]
+        gpsimd_tiles = [(0, 0), (0, 1), (0, 2), (0, 3)]
         y_sb = new_tile([P, len(gpsimd_tiles), M_OUT], F32, "y_sb", "raw20_0")
-        skipped = [new_tile([P, 2, M_OUT], F32, f"skipped{b}", f"x_rows{b}") for b in range(BLOCKS)]
+        first_term = new_tile([P, M_OUT], F32, "first_term", "x_rows0")
+        terms = new_tile([P, 3, M_OUT], F32, "terms", "w2_planes")
 
         def finish_gpsimd(b, t):
             n = gpsimd_tiles.index((b, t))
-            term = skipped[n // 2][:, n % 2, :]
-            if n < 2:
+            term = terms[:, n - 1, :] if n else first_term[:]
+            if n < 1:
                 nc.gpsimd.tensor_scalar(term, dest[b, t], skip_sb[:, b, t : t + 1], 0.0, MULT, ADD)
             else:
                 nc.scalar.activation(term, dest[b, t], COPY, scale=skip_sb[:, b, t : t + 1])
             nc.scalar.copy(y_sb[:, n, :], y_banks[b * PACK + t][:])
             nc.gpsimd.tensor_tensor(result[b][:, t, :], term, y_sb[:, n, :], ADD)
-            nc.sync.dma_start(out_rows[b, t], result[b][:, t, :])
 
         def finish_vector(b, t, parts):
             for n in range(parts):
@@ -314,13 +320,12 @@ def tile_list_ringing_residual_layer_kernel(
                 )
                 nc.sync.dma_start(out_rows[b, t][:, cols], result[b][:, t, cols])
 
-        finish_vector(0, 3, 1)
-        finish_gpsimd(0, 0)
+        for b, t in gpsimd_tiles:
+            finish_gpsimd(b, t)
+        for b, t in gpsimd_tiles:
+            nc.scalar.dma_start(out_rows[b, t], result[b][:, t, :])
         finish_vector(1, 0, 1)
-        pick_dest(1, 2, dest[1, 0])
-        finish_gpsimd(0, 1)
         finish_vector(1, 1, 1)
-        pick_dest(1, 3, dest[1, 1])
-        finish_gpsimd(0, 2)
+        pick_dest(1, 3, dest[1, 0])
         finish_vector(1, 2, 1)
         finish_vector(1, 3, 2)

@@ -246,7 +246,9 @@ def tile_list_ringing_residual_layer_kernel(
             w2_codes[:].bitcast(U16).rearrange("p (g t m) -> p g t m", t=PACK, m=P),
             w2_raw[:].rearrange("p a c -> p (a c)").bitcast(U16).rearrange("p (g m t) -> p g t m", t=PACK, m=P),
         )
-        pick_dest(0, 0, new_tile([P, M_OUT], F32, "dest00", "w1_codes201")[:])
+        early_picks = new_tile([P, 2, M_OUT], F32, "early_picks", "w1_codes201")
+        for t in range(2):
+            pick_dest(0, t, early_picks[:, t, :])
 
         def quantise_x(b, scalar_cols):
             x_grouped = new_tile([P, M_OUT, PACK], BF16, f"x_grouped{b}")
@@ -270,15 +272,13 @@ def tile_list_ringing_residual_layer_kernel(
             activate(1, t)
         quantise_x(1, 320)
         middle_picks = new_tile([P, 3, M_OUT], F32, "middle_picks", "source11")
-        for n, (b, t) in enumerate([(0, 1), (0, 2), (0, 3)]):
+        for n, (b, t) in enumerate([(0, 2), (0, 3), (1, 0)]):
             pick_dest(b, t, middle_picks[:, n, :])
-        late_picks = new_tile([P, 3, M_OUT], F32, "late_picks", "x_rows1")
-        for t in range(3):
-            pick_dest(1, t, late_picks[:, t, :])
+        pick_dest(1, 1, new_tile([P, M_OUT], F32, "dest11", "x_rows1")[:])
 
         y_banks = [psum.tile([P, BANK], F32, name=f"y_bank{i}", tag=f"bank{i}") for i in range(BLOCKS * PACK)]
         for a in range(BLOCKS):
-            for i in range(BLOCKS * PACK):
+            for i in [0, 3, 4, 1, 2, 5, 6, 7]:
                 c0 = a * H + i * P
                 nc.tensor.matmul_mx(
                     out=y_banks[i][:],
@@ -292,10 +292,10 @@ def tile_list_ringing_residual_layer_kernel(
 
         out_rows = out.rearrange("(b p t) m -> b t p m", p=P, t=PACK)
         result = [new_tile([P, PACK, M_OUT], F32, f"result{b}", f"raw{b}0") for b in range(BLOCKS)]
-        gpsimd_tiles = [(0, 0), (0, 1), (0, 2), (0, 3)]
+        gpsimd_tiles = [(0, 0), (0, 1), (0, 2)]
         y_sb = new_tile([P, len(gpsimd_tiles), M_OUT], F32, "y_sb", "raw20_0")
         first_term = new_tile([P, M_OUT], F32, "first_term", "x_rows0")
-        terms = new_tile([P, 3, M_OUT], F32, "terms", "w2_planes")
+        terms = new_tile([P, 2, M_OUT], F32, "terms", "w2_planes")
 
         def finish_gpsimd(b, t):
             n = gpsimd_tiles.index((b, t))
@@ -324,7 +324,9 @@ def tile_list_ringing_residual_layer_kernel(
             finish_gpsimd(b, t)
         for b, t in gpsimd_tiles:
             nc.scalar.dma_start(out_rows[b, t], result[b][:, t, :])
+        finish_vector(0, 3, 1)
         finish_vector(1, 0, 1)
+        pick_dest(1, 2, dest[0, 3])
         finish_vector(1, 1, 1)
         pick_dest(1, 3, dest[1, 0])
         finish_vector(1, 2, 1)

@@ -33,10 +33,14 @@ def tile_list_ringing_residual_layer_kernel(
     with ExitStack() as ctx:
         lists = ctx.enter_context(tc.tile_pool(name="lists", bufs=1))
         sb = ctx.enter_context(tc.tile_pool(name="sb", bufs=1))
+        late = ctx.enter_context(tc.tile_pool(name="late", bufs=1))
         psum = ctx.enter_context(tc.psum_pool(name="psum", bufs=1))
 
         def new_tile(shape, dtype, name, tag=None):
             return sb.tile(shape, dtype, name=name, tag=tag or name, align_bytes=64)
+
+        def placed_tile(shape, dtype, name, kib):
+            return late.tile(shape, dtype, name=name, offset=1024 * kib, align_bytes=64)
 
         offs_sb = lists.tile([P, S // 16], U16, name="offs_sb")
         pos1_sb = lists.tile([P, M_OUT // 16], U16, name="pos1_sb")
@@ -58,7 +62,10 @@ def tile_list_ringing_residual_layer_kernel(
             nc.sync.dma_start(tab[a][:], tab_words[a].rearrange("p t i -> p (t i)").bitcast(I32))
 
         def load_w1(a, b):
-            raw[a, b] = new_tile([P, PACK, K_PASS], F32, f"raw{a}{b}")
+            if b:
+                raw[a, b] = placed_tile([P, PACK, K_PASS], F32, f"raw{a}{b}", 8 * (a - 1))
+            else:
+                raw[a, b] = new_tile([P, PACK, K_PASS], F32, f"raw{a}{b}")
             rows = w1[a * K_PASS : (a + 1) * K_PASS, b * K_PASS : (b + 1) * K_PASS]
             nc.sync.dma_start(raw[a, b][:], rows.rearrange("(p j) c -> p j c", j=PACK))
 
@@ -84,16 +91,19 @@ def tile_list_ringing_residual_layer_kernel(
             rows = w1[2 * K_PASS : 3 * K_PASS, n * half : (n + 1) * half]
             nc.sync.dma_start(raw20[n][:], rows.rearrange("(p j) c -> p j c", j=PACK))
         nc.sync.dma_start(pos1_sb[:], pos1)
-        load_w1(0, 1)
+        raw01 = [new_tile([P, PACK, half], F32, f"raw01_{n}") for n in range(2)]
+        for n in range(2):
+            rows = w1[0:K_PASS, K_PASS + n * half : K_PASS + (n + 1) * half]
+            nc.sync.dma_start(raw01[n][:], rows.rearrange("(p j) c -> p j c", j=PACK))
         nc.sync.dma_start(pos2_sb[:], pos2)
+        w2_raw = new_tile([P, BLOCKS, H // 2], I32, "w2_raw")
+        nc.sync.dma_start(w2_raw[:], w2_words.bitcast(I32).rearrange("a p c -> p a c"))
         load_w1(1, 1)
         gain_sb = new_tile([P, BLOCKS, PACK], F32, "gain_sb")
         nc.gpsimd.dma_start(gain_sb[:], gain.rearrange("(b p t) -> p b t", p=P, t=PACK))
         load_w1(2, 1)
         skip_sb = new_tile([P, BLOCKS, PACK], F32, "skip_sb")
         nc.gpsimd.dma_start(skip_sb[:], skip.rearrange("(b p t) -> p b t", p=P, t=PACK))
-        w2_raw = new_tile([P, BLOCKS, H // 2], I32, "w2_raw")
-        nc.sync.dma_start(w2_raw[:], w2_words.bitcast(I32).rearrange("a p c -> p a c"))
 
         picked = {}
         picked_planes = new_tile([P, S], U8, "picked_planes")
@@ -164,8 +174,13 @@ def tile_list_ringing_residual_layer_kernel(
                 nc.scalar.copy(h[b][:, t, u * BANK : (u + 1) * BANK], banks[b, t, u][:])
 
         def pick_source(b, t):
-            source[b, t] = new_tile([P, M_OUT], F32, f"source{b}{t}", {(0, 0): "raw01", (0, 2): "w1_codes202", (0, 3): "tab1"}.get((b, t)))
-            nc.vector.tensor_copy(source[b, t][:], h[b][:, t, :].indirect(pos1_sb[:]))
+            if b == 0 and t < PACK - 1:
+                source[b, t] = first_picks[:, t, :]
+            elif (b, t) == (1, 1):
+                source[b, t] = placed_tile([P, M_OUT], F32, "source11", 22)[:]
+            else:
+                source[b, t] = new_tile([P, M_OUT], F32, f"source{b}{t}", None if b else "tab1")[:]
+            nc.vector.tensor_copy(source[b, t], h[b][:, t, :].indirect(pos1_sb[:]))
 
         def pick_dest(b, t, picks):
             dest[b, t] = picks
@@ -200,35 +215,46 @@ def tile_list_ringing_residual_layer_kernel(
         for t in range(PACK):
             first_product(2, 0, t)
             empty_banks(0, t)
-        interleave_w1(nc.vector.tensor_copy, 0, 1)
+        grouped[0, 1] = new_tile([P, PACK, P, PACK], BF16, "grouped01")
+        for n in range(2):
+            interleave(nc.vector.tensor_copy, grouped[0, 1], raw01[n][:], n * P // 2, P // 2)
+        first_picks = new_tile([P, PACK, M_OUT], F32, "first_picks", "raw01_1")
         quantise_w1(0, 1, 0, grouped[0, 1][:])
-        for t in range(2):
+        w2_codes = new_tile([P, BLOCKS * 2 * H], U8, "w2_codes", "grouped01")
+        w2_bytes = w2_raw[:].rearrange("p a c -> p (a c)").bitcast(U8)
+        for g in range(BLOCKS * BLOCKS):
+            group = slice(g * 2 * K_PASS, (g + 1) * 2 * K_PASS)
+            nc.gpsimd.tensor_copy(
+                w2_codes[:, group].rearrange("p (t m e) -> p t m e", t=PACK, e=2),
+                w2_bytes[:, group].rearrange("p (m t e) -> p t m e", t=PACK, e=2),
+            )
+        for t in range(PACK):
             pick_source(0, t)
+        pick_dest(0, 0, first_picks[:, PACK - 1, :])
 
-        def prepare_in_pairs(a, b, tags):
-            for i, tag in enumerate(tags):
-                pair = new_tile([P, 2, P, PACK], BF16, f"pair{a}{b}{i}", tag)
-                nc.scalar.copy(
-                    pair[:].rearrange("p h m j -> p m j h"),
-                    raw[a, b][:].rearrange("p j (m i h) -> p i m j h", i=2, h=2)[:, i],
-                )
-                quantise_w1(a, b, 2 * i, pair[:])
+        def prepare_pair(a, b, i, tag):
+            pair = new_tile([P, 2, P, PACK], BF16, f"pair{a}{b}{i}", tag)
+            nc.scalar.copy(
+                pair[:].rearrange("p h m j -> p m j h"),
+                raw[a, b][:].rearrange("p j (m i h) -> p i m j h", i=2, h=2)[:, i],
+            )
+            quantise_w1(a, b, 2 * i, pair[:])
 
-        prepare_in_pairs(1, 1, ["w1_codes202", "w1_planes202"])
-        for t in range(2, PACK):
-            pick_source(0, t)
-        prepare_in_pairs(2, 1, ["w1_codes200", "w1_codes201"])
+        prepare_pair(1, 1, 0, "w1_codes202")
+        prepare_pair(1, 1, 1, "w1_planes202")
+        prepare_pair(2, 1, 0, "w1_codes200")
+        prepare_pair(2, 1, 1, "w1_codes201")
         for t in range(PACK):
             for a in range(K_PASSES):
                 first_product(a, 1, t)
-        act = [new_tile([P, PACK, M_OUT], F32, "act0", "raw21")]
-        x_rows = [new_tile([P, PACK, M_OUT], BF16, f"x_rows{b}") for b in range(BLOCKS)]
+        act = [placed_tile([P, PACK, M_OUT], F32, "act0", 10)]
+        x_rows = [placed_tile([P, PACK, M_OUT], BF16, "x_rows0", 18), new_tile([P, PACK, M_OUT], BF16, "x_rows1")]
         x_codes = [new_tile([P, M_OUT], U32, f"x_codes{b}", ["source10", None][b]) for b in range(BLOCKS)]
         x_planes = [new_tile([P, M_OUT], U8, f"x_planes{b}") for b in range(BLOCKS)]
 
         def activate(b, t):
             silu = act[b][:, t, :]
-            nc.scalar.activation(silu, source[b, t][:], SILU, bias=silu_bias[:])
+            nc.scalar.activation(silu, source[b, t], SILU, bias=silu_bias[:])
             if (b, t) == (BLOCKS - 1, PACK - 1):
                 nc.scalar.activation(x_rows[b][:, t, :], silu, COPY, scale=gain_sb[:, b, t : t + 1])
             else:
@@ -241,14 +267,9 @@ def tile_list_ringing_residual_layer_kernel(
             empty_banks(1, t)
             pick_source(1, t)
 
-        w2_codes = new_tile([P, BLOCKS * 2 * H], U8, "w2_codes", "w1_codes200")
-        nc.vector.tensor_copy(
-            w2_codes[:].bitcast(U16).rearrange("p (g t m) -> p g t m", t=PACK, m=P),
-            w2_raw[:].rearrange("p a c -> p (a c)").bitcast(U16).rearrange("p (g m t) -> p g t m", t=PACK, m=P),
-        )
-        early_picks = new_tile([P, 2, M_OUT], F32, "early_picks", "w1_codes201")
-        for t in range(2):
-            pick_dest(0, t, early_picks[:, t, :])
+        pick_dest(0, 1, placed_tile([P, M_OUT], F32, "dest01", 4)[:])
+        pick_dest(0, 2, placed_tile([P, M_OUT], F32, "dest02", 0)[:])
+        pick_dest(0, 3, placed_tile([P, M_OUT], F32, "dest03", 8)[:])
 
         def quantise_x(b, scalar_cols):
             x_grouped = new_tile([P, M_OUT, PACK], BF16, f"x_grouped{b}")
@@ -271,10 +292,10 @@ def tile_list_ringing_residual_layer_kernel(
         for t in range(PACK):
             activate(1, t)
         quantise_x(1, 320)
-        middle_picks = new_tile([P, 3, M_OUT], F32, "middle_picks", "source11")
-        for n, (b, t) in enumerate([(0, 2), (0, 3), (1, 0)]):
+        middle_picks = placed_tile([P, 2, M_OUT], F32, "middle_picks", 21)
+        for n, (b, t) in enumerate([(1, 0), (1, 1)]):
             pick_dest(b, t, middle_picks[:, n, :])
-        pick_dest(1, 1, new_tile([P, M_OUT], F32, "dest11", "x_rows1")[:])
+        pick_dest(1, 2, new_tile([P, M_OUT], F32, "dest12", "x_rows1")[:])
 
         y_banks = [psum.tile([P, BANK], F32, name=f"y_bank{i}", tag=f"bank{i}") for i in range(BLOCKS * PACK)]
         for a in range(BLOCKS):
@@ -294,7 +315,7 @@ def tile_list_ringing_residual_layer_kernel(
         result = [new_tile([P, PACK, M_OUT], F32, f"result{b}", f"raw{b}0") for b in range(BLOCKS)]
         gpsimd_tiles = [(0, 0), (0, 1), (0, 2)]
         y_sb = new_tile([P, len(gpsimd_tiles), M_OUT], F32, "y_sb", "raw20_0")
-        first_term = new_tile([P, M_OUT], F32, "first_term", "x_rows0")
+        first_term = placed_tile([P, M_OUT], F32, "first_term", 18)
         terms = new_tile([P, 2, M_OUT], F32, "terms", "w2_planes")
 
         def finish_gpsimd(b, t):
@@ -326,7 +347,6 @@ def tile_list_ringing_residual_layer_kernel(
             nc.scalar.dma_start(out_rows[b, t], result[b][:, t, :])
         finish_vector(0, 3, 1)
         finish_vector(1, 0, 1)
-        pick_dest(1, 2, dest[0, 3])
         finish_vector(1, 1, 1)
         pick_dest(1, 3, dest[1, 0])
         finish_vector(1, 2, 1)

@@ -96,7 +96,7 @@ def tile_list_ringing_residual_layer_kernel(
             rows = w1[0:K_PASS, K_PASS + n * half : K_PASS + (n + 1) * half]
             nc.sync.dma_start(raw01[n][:], rows.rearrange("(p j) c -> p j c", j=PACK))
         nc.sync.dma_start(pos2_sb[:], pos2)
-        w2_raw = new_tile([P, BLOCKS, H // 2], I32, "w2_raw")
+        w2_raw = placed_tile([P, BLOCKS, H // 2], I32, "w2_raw", 18)
         nc.sync.dma_start(w2_raw[:], w2_words.bitcast(I32).rearrange("a p c -> p a c"))
         load_w1(1, 1)
         gain_sb = new_tile([P, BLOCKS, PACK], F32, "gain_sb")
@@ -176,8 +176,6 @@ def tile_list_ringing_residual_layer_kernel(
         def pick_source(b, t):
             if b == 0 and t < PACK - 1:
                 source[b, t] = first_picks[:, t, :]
-            elif (b, t) == (1, 1):
-                source[b, t] = placed_tile([P, M_OUT], F32, "source11", 22)[:]
             else:
                 source[b, t] = new_tile([P, M_OUT], F32, f"source{b}{t}", None if b else "tab1")[:]
             nc.vector.tensor_copy(source[b, t], h[b][:, t, :].indirect(pos1_sb[:]))
@@ -215,12 +213,12 @@ def tile_list_ringing_residual_layer_kernel(
         for t in range(PACK):
             first_product(2, 0, t)
             empty_banks(0, t)
-        grouped[0, 1] = new_tile([P, PACK, P, PACK], BF16, "grouped01")
+        grouped[0, 1] = new_tile([P, PACK, P, PACK], BF16, "grouped01", "raw20_1")
         for n in range(2):
             interleave(nc.vector.tensor_copy, grouped[0, 1], raw01[n][:], n * P // 2, P // 2)
         first_picks = new_tile([P, PACK, M_OUT], F32, "first_picks", "raw01_1")
         quantise_w1(0, 1, 0, grouped[0, 1][:])
-        w2_codes = new_tile([P, BLOCKS * 2 * H], U8, "w2_codes", "grouped01")
+        w2_codes = new_tile([P, BLOCKS * 2 * H], U8, "w2_codes", "raw20_1")
         w2_bytes = w2_raw[:].rearrange("p a c -> p (a c)").bitcast(U8)
         for g in range(BLOCKS * BLOCKS):
             group = slice(g * 2 * K_PASS, (g + 1) * 2 * K_PASS)
@@ -248,7 +246,7 @@ def tile_list_ringing_residual_layer_kernel(
             for a in range(K_PASSES):
                 first_product(a, 1, t)
         act = [placed_tile([P, PACK, M_OUT], F32, "act0", 10)]
-        x_rows = [placed_tile([P, PACK, M_OUT], BF16, "x_rows0", 18), new_tile([P, PACK, M_OUT], BF16, "x_rows1")]
+        x_rows = [placed_tile([P, PACK, M_OUT], BF16, "x_rows0", 18), placed_tile([P, PACK, M_OUT], BF16, "x_rows1", 20)]
         x_codes = [new_tile([P, M_OUT], U32, f"x_codes{b}", ["source10", None][b]) for b in range(BLOCKS)]
         x_planes = [new_tile([P, M_OUT], U8, f"x_planes{b}") for b in range(BLOCKS)]
 
@@ -292,10 +290,10 @@ def tile_list_ringing_residual_layer_kernel(
         for t in range(PACK):
             activate(1, t)
         quantise_x(1, 320)
-        middle_picks = placed_tile([P, 2, M_OUT], F32, "middle_picks", 21)
+        middle_picks = new_tile([P, 2, M_OUT], F32, "middle_picks", "x_grouped0")
         for n, (b, t) in enumerate([(1, 0), (1, 1)]):
             pick_dest(b, t, middle_picks[:, n, :])
-        pick_dest(1, 2, new_tile([P, M_OUT], F32, "dest12", "x_rows1")[:])
+        pick_dest(1, 2, placed_tile([P, M_OUT], F32, "dest12", 20)[:])
 
         y_banks = [psum.tile([P, BANK], F32, name=f"y_bank{i}", tag=f"bank{i}") for i in range(BLOCKS * PACK)]
         for a in range(BLOCKS):

@@ -266,8 +266,7 @@ def tile_list_ringing_residual_layer_kernel(
             pick_source(1, t)
 
         pick_dest(0, 1, placed_tile([P, M_OUT], F32, "dest01", 4)[:])
-        pick_dest(0, 2, placed_tile([P, M_OUT], F32, "dest02", 0)[:])
-        pick_dest(0, 3, placed_tile([P, M_OUT], F32, "dest03", 8)[:])
+        pick_dest(0, 2, placed_tile([P, M_OUT], F32, "dest02", 8)[:])
 
         def quantise_x(b, scalar_cols):
             x_grouped = new_tile([P, M_OUT, PACK], BF16, f"x_grouped{b}")
@@ -290,8 +289,8 @@ def tile_list_ringing_residual_layer_kernel(
         for t in range(PACK):
             activate(1, t)
         quantise_x(1, 320)
-        middle_picks = new_tile([P, 2, M_OUT], F32, "middle_picks", "x_grouped0")
-        for n, (b, t) in enumerate([(1, 0), (1, 1)]):
+        middle_picks = new_tile([P, 3, M_OUT], F32, "middle_picks", "x_grouped0")
+        for n, (b, t) in enumerate([(0, 3), (1, 0), (1, 1)]):
             pick_dest(b, t, middle_picks[:, n, :])
         pick_dest(1, 2, placed_tile([P, M_OUT], F32, "dest12", 20)[:])
 

@@ -99,11 +99,11 @@ def tile_list_ringing_residual_layer_kernel(
         w2_raw = placed_tile([P, BLOCKS, H // 2], I32, "w2_raw", 18)
         nc.sync.dma_start(w2_raw[:], w2_words.bitcast(I32).rearrange("a p c -> p a c"))
         load_w1(1, 1)
-        gain_sb = new_tile([P, BLOCKS, PACK], F32, "gain_sb")
-        nc.gpsimd.dma_start(gain_sb[:], gain.rearrange("(b p t) -> p b t", p=P, t=PACK))
         load_w1(2, 1)
+        gain_sb = new_tile([P, BLOCKS, PACK], F32, "gain_sb")
+        nc.sync.dma_start(gain_sb[:], gain.rearrange("(b p t) -> p b t", p=P, t=PACK))
         skip_sb = new_tile([P, BLOCKS, PACK], F32, "skip_sb")
-        nc.gpsimd.dma_start(skip_sb[:], skip.rearrange("(b p t) -> p b t", p=P, t=PACK))
+        nc.sync.dma_start(skip_sb[:], skip.rearrange("(b p t) -> p b t", p=P, t=PACK))
 
         picked = {}
         picked_planes = new_tile([P, S], U8, "picked_planes")

@@ -52,7 +52,7 @@ def tile_list_ringing_residual_layer_kernel(
         nc.vector.memset(zero[:], 0.0)
         silu_bias = new_tile([P, 1], F32, "silu_bias")
         nc.scalar.activation(silu_bias[:], zero[:], SILU)
-        w2_planes = new_tile([P, BLOCKS * H], U8, "w2_planes")
+        w2_planes = placed_tile([P, BLOCKS * H], U8, "w2_planes", 26)
         nc.vector.memset(w2_planes[:].bitcast(I32), 0)
 
         tab = [new_tile([P, T], I32, f"tab{a}") for a in range(K_PASSES)]
@@ -114,8 +114,7 @@ def tile_list_ringing_residual_layer_kernel(
             for u in range(2):
                 picked[a, u] = words[:, u * BANK : (u + 1) * BANK]
 
-        def pick_words_half(a, u, tag):
-            words = new_tile([P, BANK], U32, f"picked{a}{u}", tag)
+        def pick_words_half(a, u, words):
             entries = offs_sb[:, u * BANK // 16 : (u + 1) * BANK // 16]
             nc.vector.tensor_copy(words[:], tab[a][:].bitcast(U32).indirect(entries))
             picked[a, u] = words[:]
@@ -137,9 +136,10 @@ def tile_list_ringing_residual_layer_kernel(
             grouped[a, b] = new_tile([P, PACK, P, PACK], BF16, f"grouped{a}{b}")
             interleave(copy, grouped[a, b], raw[a, b][:], 0, P)
 
-        def quantise_w1(a, b, first, words):
+        def quantise_w1(a, b, first, words, codes=None):
             count = words.shape[1]
-            codes = new_tile([P, count * P], U32, f"w1_codes{a}{b}{first}")
+            if codes is None:
+                codes = new_tile([P, count * P], U32, f"w1_codes{a}{b}{first}")
             planes = new_tile([P, count * P], U8, f"w1_planes{a}{b}{first}")
             nc.vector.quantize_mx(
                 out=codes[:].bitcast(FP8X4), scales=planes[:], in_=words.rearrange("p t m j -> p (t m j)")
@@ -192,20 +192,23 @@ def tile_list_ringing_residual_layer_kernel(
             first_product(0, 0, t)
         pick_words(1)
         interleave_w1(nc.scalar.copy, 1, 0)
-        quantise_w1(1, 0, 0, grouped[1, 0][:])
-        for t in range(PACK):
+        quantise_w1(1, 0, 0, grouped[1, 0][:, 0:2])
+        for t in range(2):
             first_product(1, 0, t)
         w2_sorted_planes = new_tile([P, BLOCKS * H], U8, "w2_sorted_planes")
         nc.vector.tensor_copy(
             w2_sorted_planes[:].rearrange("p (g t m) -> p g t m", t=PACK, m=P),
             w2_planes[:].rearrange("p (g m t) -> p g t m", t=PACK, m=P),
         )
-        pick_words_half(2, 0, "tab_planes")
-        pick_words_half(2, 1, "w2_planes")
+        pick_words_half(2, 0, new_tile([P, BANK], U32, "picked20", "tab_planes"))
+        quantise_w1(1, 0, 2, grouped[1, 0][:, 2:4], placed_tile([P, 2 * P], U32, "w1_codes102", 26))
+        for t in range(2, PACK):
+            first_product(1, 0, t)
+        pick_words_half(2, 1, placed_tile([P, BANK], U32, "picked21", 27))
         grouped[2, 0] = new_tile([P, PACK, P, PACK], BF16, "grouped20")
         interleave(nc.scalar.copy, grouped[2, 0], raw20[0][:], 0, P // 2)
-        interleave(nc.vector.tensor_copy, grouped[2, 0], raw20[1][:, :, 0 : PACK * 40], P // 2, 40)
-        interleave(nc.scalar.copy, grouped[2, 0], raw20[1][:, :, PACK * 40 : PACK * 64], P // 2 + 40, 24)
+        interleave(nc.vector.tensor_copy, grouped[2, 0], raw20[1][:, :, 0 : PACK * 48], P // 2, 48)
+        interleave(nc.scalar.copy, grouped[2, 0], raw20[1][:, :, PACK * 48 : PACK * 64], P // 2 + 48, 16)
         quantise_w1(2, 0, 0, grouped[2, 0][:, 0:1])
         quantise_w1(2, 0, 1, grouped[2, 0][:, 1:2])
         quantise_w1(2, 0, 2, grouped[2, 0][:, 2:4])
@@ -285,7 +288,7 @@ def tile_list_ringing_residual_layer_kernel(
             )
 
         quantise_x(0, 0)
-        act.append(new_tile([P, PACK, M_OUT], F32, "act1", "w2_planes"))
+        act.append(placed_tile([P, PACK, M_OUT], F32, "act1", 27))
         for t in range(PACK):
             activate(1, t)
         quantise_x(1, 320)
@@ -313,7 +316,7 @@ def tile_list_ringing_residual_layer_kernel(
         gpsimd_tiles = [(0, 0), (0, 1), (0, 2)]
         y_sb = new_tile([P, len(gpsimd_tiles), M_OUT], F32, "y_sb", "raw20_0")
         first_term = placed_tile([P, M_OUT], F32, "first_term", 18)
-        terms = new_tile([P, 2, M_OUT], F32, "terms", "w2_planes")
+        terms = placed_tile([P, 2, M_OUT], F32, "terms", 27)
 
         def finish_gpsimd(b, t):
             n = gpsimd_tiles.index((b, t))

from contextlib import ExitStack

import concourse.mybir as mybir

K, H, T, S, M_OUT = 1536, 1024, 4096, 1024, 512
FLOPS = 2 * K * H * S + 2 * H * H * M_OUT

F32 = mybir.dt.float32
BF16 = mybir.dt.bfloat16
I32 = mybir.dt.int32
U32 = mybir.dt.uint32
U16 = mybir.dt.uint16
U8 = mybir.dt.uint8
FP8X4 = mybir.dt.float8_e4m3fn_x4
FP4X4 = mybir.dt.float4_e2m1fn_x4
SILU = mybir.ActivationFunctionType.Silu
COPY = mybir.ActivationFunctionType.Copy
MULT = mybir.AluOpType.mult
ADD = mybir.AluOpType.add

P = 128
PACK = 4
K_PASS = P * PACK
BANK = 512
K_PASSES = K // K_PASS
BLOCKS = H // K_PASS


def tile_list_ringing_residual_layer_kernel(
    tc, tab_words, tab_scales, offs, w1, pos1, gain, w2_words, w2_scales, pos2, skip, out
):
    nc = tc.nc
    with ExitStack() as ctx:
        lists = ctx.enter_context(tc.tile_pool(name="lists", bufs=1))
        sb = ctx.enter_context(tc.tile_pool(name="sb", bufs=1))
        late = ctx.enter_context(tc.tile_pool(name="late", bufs=1))
        psum = ctx.enter_context(tc.psum_pool(name="psum", bufs=1))

        def new_tile(shape, dtype, name, tag=None):
            return sb.tile(shape, dtype, name=name, tag=tag or name, align_bytes=64)

        def placed_tile(shape, dtype, name, kib):
            return late.tile(shape, dtype, name=name, offset=1024 * kib, align_bytes=64)

        offs_sb = lists.tile([P, S // 16], U16, name="offs_sb")
        pos1_sb = lists.tile([P, M_OUT // 16], U16, name="pos1_sb")
        pos2_sb = lists.tile([P, M_OUT // 16], U16, name="pos2_sb")

        tab_planes = new_tile([P, T], U8, "tab_planes")
        nc.vector.memset(tab_planes[:].bitcast(I32), 0)
        zero = new_tile([P, 1], F32, "zero")
        nc.vector.memset(zero[:], 0.0)
        silu_bias = new_tile([P, 1], F32, "silu_bias")
        nc.scalar.activation(silu_bias[:], zero[:], SILU)
        w2_planes = placed_tile([P, BLOCKS * H], U8, "w2_planes", 26)
        nc.vector.memset(w2_planes[:].bitcast(I32), 0)

        tab = [new_tile([P, T], I32, f"tab{a}") for a in range(K_PASSES)]
        raw = {}

        def load_tab(a):
            nc.sync.dma_start(tab[a][:], tab_words[a].rearrange("p t i -> p (t i)").bitcast(I32))

        def load_w1(a, b):
            if b:
                raw[a, b] = placed_tile([P, PACK, K_PASS], F32, f"raw{a}{b}", 8 * (a - 1))
            else:
                raw[a, b] = new_tile([P, PACK, K_PASS], F32, f"raw{a}{b}")
            rows = w1[a * K_PASS : (a + 1) * K_PASS, b * K_PASS : (b + 1) * K_PASS]
            nc.sync.dma_start(raw[a, b][:], rows.rearrange("(p j) c -> p j c", j=PACK))

        load_tab(0)
        nc.sync.dma_start(offs_sb[:], offs)
        load_w1(0, 0)
        for q in range(4):
            nc.gpsimd.dma_start(
                tab_planes[32 * q + 4 : 32 * q + 4 + 4 * K_PASSES, :].bitcast(I32),
                tab_scales[:, 4 * q : 4 * q + 4, :].bitcast(I32),
            )
        load_tab(1)
        load_w1(1, 0)
        for q in range(4):
            nc.gpsimd.dma_start(
                w2_planes[32 * q : 32 * q + 4, :].bitcast(I32).rearrange("r (a c) -> r a c", a=BLOCKS),
                w2_scales[:, 4 * q : 4 * q + 4, :].bitcast(I32).rearrange("a r c -> r a c"),
            )
        load_tab(2)
        half = K_PASS // 2
        raw20 = [new_tile([P, PACK, half], F32, f"raw20_{n}") for n in range(2)]
        for n in range(2):
            rows = w1[2 * K_PASS : 3 * K_PASS, n * half : (n + 1) * half]
            nc.sync.dma_start(raw20[n][:], rows.rearrange("(p j) c -> p j c", j=PACK))
        nc.sync.dma_start(pos1_sb[:], pos1)
        raw01 = [new_tile([P, PACK, half], F32, f"raw01_{n}") for n in range(2)]
        for n in range(2):
            rows = w1[0:K_PASS, K_PASS + n * half : K_PASS + (n + 1) * half]
            nc.sync.dma_start(raw01[n][:], rows.rearrange("(p j) c -> p j c", j=PACK))
        nc.sync.dma_start(pos2_sb[:], pos2)
        w2_raw = placed_tile([P, BLOCKS, H // 2], I32, "w2_raw", 18)
        nc.sync.dma_start(w2_raw[:], w2_words.bitcast(I32).rearrange("a p c -> p a c"))
        load_w1(1, 1)
        load_w1(2, 1)
        gain_sb = new_tile([P, BLOCKS, PACK], F32, "gain_sb")
        nc.sync.dma_start(gain_sb[:], gain.rearrange("(b p t) -> p b t", p=P, t=PACK))
        skip_sb = new_tile([P, BLOCKS, PACK], F32, "skip_sb")
        nc.sync.dma_start(skip_sb[:], skip.rearrange("(b p t) -> p b t", p=P, t=PACK))

        picked = {}
        picked_planes = new_tile([P, S], U8, "picked_planes")

        def pick_words(a):
            words = new_tile([P, S], U32, f"picked{a}")
            nc.vector.tensor_copy(words[:], tab[a][:].bitcast(U32).indirect(offs_sb[:]))
            for u in range(2):
                picked[a, u] = words[:, u * BANK : (u + 1) * BANK]

        def pick_words_half(a, u, words):
            entries = offs_sb[:, u * BANK // 16 : (u + 1) * BANK // 16]
            nc.vector.tensor_copy(words[:], tab[a][:].bitcast(U32).indirect(entries))
            picked[a, u] = words[:]

        def gpsimd_copy(dst, src):
            nc.gpsimd.tensor_scalar(dst, src, 1.0, 0.0, MULT, ADD)

        grouped = {}
        w1_codes = {}
        w1_planes = {}

        def interleave(copy, dst, src, m0, count):
            copy(
                dst[:, :, m0 : m0 + count, :].rearrange("p (i h) m j -> p i m j h", h=2),
                src.rearrange("p j (m i h) -> p i m j h", i=2, h=2),
            )

        def interleave_w1(copy, a, b):
            grouped[a, b] = new_tile([P, PACK, P, PACK], BF16, f"grouped{a}{b}")
            interleave(copy, grouped[a, b], raw[a, b][:], 0, P)

        def quantise_w1(a, b, first, words, codes=None):
            count = words.shape[1]
            if codes is None:
                codes = new_tile([P, count * P], U32, f"w1_codes{a}{b}{first}")
            planes = new_tile([P, count * P], U8, f"w1_planes{a}{b}{first}")
            nc.vector.quantize_mx(
                out=codes[:].bitcast(FP8X4), scales=planes[:], in_=words.rearrange("p t m j -> p (t m j)")
            )
            for n in range(count):
                w1_codes[a, b, first + n] = codes[:, n * P : (n + 1) * P]
                w1_planes[a, b, first + n] = planes[:, n * P : (n + 1) * P]

        banks = {}

        def first_product(a, b, t):
            for u in range(2):
                if a == 0:
                    banks[b, t, u] = psum.tile([P, BANK], F32, name=f"h_bank{b}{t}{u}", tag=f"bank{2 * t + u}")
                cols = slice(u * BANK, (u + 1) * BANK)
                nc.tensor.matmul_mx(
                    out=banks[b, t, u][:],
                    lhsT=w1_codes[a, b, t].bitcast(FP8X4),
                    lhsT_scale=w1_planes[a, b, t],
                    rhs=picked[a, u].bitcast(FP8X4),
                    rhs_scale=picked_planes[4 * (a + 1) : P, cols],
                    start=(a == 0),
                    stop=(a == K_PASSES - 1),
                )

        h = []
        source = {}
        dest = {}

        def empty_banks(b, t):
            for u in range(2):
                nc.scalar.copy(h[b][:, t, u * BANK : (u + 1) * BANK], banks[b, t, u][:])

        def pick_source(b, t):
            if b == 0 and t < PACK - 1:
                source[b, t] = first_picks[:, t, :]
            else:
                source[b, t] = new_tile([P, M_OUT], F32, f"source{b}{t}", None if b else "tab1")[:]
            nc.vector.tensor_copy(source[b, t], h[b][:, t, :].indirect(pos1_sb[:]))

        def pick_dest(b, t, picks):
            dest[b, t] = picks
            nc.vector.tensor_copy(picks, h[b][:, t, :].indirect(pos2_sb[:]))

        nc.vector.tensor_copy(picked_planes[:], tab_planes[:].indirect(offs_sb[:]))
        pick_words(0)
        interleave_w1(nc.scalar.copy, 0, 0)
        quantise_w1(0, 0, 0, grouped[0, 0][:])
        for t in range(PACK):
            first_product(0, 0, t)
        pick_words(1)
        interleave_w1(nc.scalar.copy, 1, 0)
        quantise_w1(1, 0, 0, grouped[1, 0][:, 0:2])
        for t in range(2):
            first_product(1, 0, t)
        w2_sorted_planes = new_tile([P, BLOCKS * H], U8, "w2_sorted_planes")
        nc.vector.tensor_copy(
            w2_sorted_planes[:].rearrange("p (g t m) -> p g t m", t=PACK, m=P),
            w2_planes[:].rearrange("p (g m t) -> p g t m", t=PACK, m=P),
        )
        pick_words_half(2, 0, new_tile([P, BANK], U32, "picked20", "tab_planes"))
        quantise_w1(1, 0, 2, grouped[1, 0][:, 2:4], placed_tile([P, 2 * P], U32, "w1_codes102", 26))
        for t in range(2, PACK):
            first_product(1, 0, t)
        pick_words_half(2, 1, placed_tile([P, BANK], U32, "picked21", 27))
        grouped[2, 0] = new_tile([P, PACK, P, PACK], BF16, "grouped20")
        interleave(nc.scalar.copy, grouped[2, 0], raw20[0][:], 0, P // 2)
        interleave(nc.vector.tensor_copy, grouped[2, 0], raw20[1][:, :, 0 : PACK * 48], P // 2, 48)
        interleave(nc.scalar.copy, grouped[2, 0], raw20[1][:, :, PACK * 48 : PACK * 64], P // 2 + 48, 16)
        quantise_w1(2, 0, 0, grouped[2, 0][:, 0:1])
        quantise_w1(2, 0, 1, grouped[2, 0][:, 1:2])
        quantise_w1(2, 0, 2, grouped[2, 0][:, 2:4])
        h.append(new_tile([P, PACK, S], F32, "h0", "tab0"))
        for t in range(PACK):
            first_product(2, 0, t)
            empty_banks(0, t)
        grouped[0, 1] = new_tile([P, PACK, P, PACK], BF16, "grouped01", "raw20_1")
        for n in range(2):
            interleave(nc.vector.tensor_copy, grouped[0, 1], raw01[n][:], n * P // 2, P // 2)
        first_picks = new_tile([P, PACK, M_OUT], F32, "first_picks", "raw01_1")
        quantise_w1(0, 1, 0, grouped[0, 1][:])
        w2_codes = new_tile([P, BLOCKS * 2 * H], U8, "w2_codes", "raw20_1")
        w2_bytes = w2_raw[:].rearrange("p a c -> p (a c)").bitcast(U8)
        for g in range(BLOCKS * BLOCKS):
            group = slice(g * 2 * K_PASS, (g + 1) * 2 * K_PASS)
            nc.gpsimd.tensor_copy(
                w2_codes[:, group].rearrange("p (t m e) -> p t m e", t=PACK, e=2),
                w2_bytes[:, group].rearrange("p (m t e) -> p t m e", t=PACK, e=2),
            )
        for t in range(PACK):
            pick_source(0, t)
        pick_dest(0, 0, first_picks[:, PACK - 1, :])

        def prepare_pair(a, b, i, tag):
            pair = new_tile([P, 2, P, PACK], BF16, f"pair{a}{b}{i}", tag)
            nc.scalar.copy(
                pair[:].rearrange("p h m j -> p m j h"),
                raw[a, b][:].rearrange("p j (m i h) -> p i m j h", i=2, h=2)[:, i],
            )
            quantise_w1(a, b, 2 * i, pair[:])

        prepare_pair(1, 1, 0, "w1_codes202")
        prepare_pair(1, 1, 1, "w1_planes202")
        prepare_pair(2, 1, 0, "w1_codes200")
        prepare_pair(2, 1, 1, "w1_codes201")
        for t in range(PACK):
            for a in range(K_PASSES):
                first_product(a, 1, t)
        act = [placed_tile([P, PACK, M_OUT], F32, "act0", 10)]
        x_rows = [placed_tile([P, PACK, M_OUT], BF16, "x_rows0", 18), placed_tile([P, PACK, M_OUT], BF16, "x_rows1", 20)]
        x_codes = [new_tile([P, M_OUT], U32, f"x_codes{b}", ["source10", None][b]) for b in range(BLOCKS)]
        x_planes = [new_tile([P, M_OUT], U8, f"x_planes{b}") for b in range(BLOCKS)]

        def activate(b, t):
            silu = act[b][:, t, :]
            nc.scalar.activation(silu, source[b, t], SILU, bias=silu_bias[:])
            if (b, t) == (BLOCKS - 1, PACK - 1):
                nc.scalar.activation(x_rows[b][:, t, :], silu, COPY, scale=gain_sb[:, b, t : t + 1])
            else:
                nc.gpsimd.tensor_scalar(x_rows[b][:, t, :], silu, gain_sb[:, b, t : t + 1], 0.0, MULT, ADD)

        for t in range(PACK):
            activate(0, t)
        h.append(new_tile([P, PACK, S], F32, "h1", "tab1"))
        for t in range(PACK):
            empty_banks(1, t)
            pick_source(1, t)

        pick_dest(0, 1, placed_tile([P, M_OUT], F32, "dest01", 4)[:])
        pick_dest(0, 2, placed_tile([P, M_OUT], F32, "dest02", 8)[:])

        def quantise_x(b, scalar_cols):
            x_grouped = new_tile([P, M_OUT, PACK], BF16, f"x_grouped{b}")
            if scalar_cols:
                nc.scalar.copy(
                    x_grouped[:, 0:scalar_cols, :].rearrange("p (c i) t -> p c t i", i=4),
                    x_rows[b][:, :, 0:scalar_cols].rearrange("p t (c i) -> p c t i", i=4),
                )
            gpsimd_copy(
                x_grouped[:, scalar_cols:M_OUT, :], x_rows[b][:, :, scalar_cols:M_OUT].rearrange("p t c -> p c t")
            )
            nc.vector.quantize_mx(
                out=x_codes[b][:].bitcast(FP8X4),
                scales=x_planes[b][:],
                in_=x_grouped[:].rearrange("p c t -> p (c t)"),
            )

        quantise_x(0, 0)
        act.append(placed_tile([P, PACK, M_OUT], F32, "act1", 27))
        for t in range(PACK):
            activate(1, t)
        quantise_x(1, 320)
        middle_picks = new_tile([P, 3, M_OUT], F32, "middle_picks", "x_grouped0")
        for n, (b, t) in enumerate([(0, 3), (1, 0), (1, 1)]):
            pick_dest(b, t, middle_picks[:, n, :])
        pick_dest(1, 2, placed_tile([P, M_OUT], F32, "dest12", 20)[:])

        y_banks = [psum.tile([P, BANK], F32, name=f"y_bank{i}", tag=f"bank{i}") for i in range(BLOCKS * PACK)]
        for a in range(BLOCKS):
            for i in [0, 3, 4, 1, 2, 5, 6, 7]:
                c0 = a * H + i * P
                nc.tensor.matmul_mx(
                    out=y_banks[i][:],
                    lhsT=w2_codes[:, 2 * c0 : 2 * (c0 + P)].bitcast(FP4X4),
                    lhsT_scale=w2_sorted_planes[:, c0 : c0 + P],
                    rhs=x_codes[a][:].bitcast(FP8X4),
                    rhs_scale=x_planes[a][:],
                    start=(a == 0),
                    stop=(a == BLOCKS - 1),
                )

        out_rows = out.rearrange("(b p t) m -> b t p m", p=P, t=PACK)
        result = [new_tile([P, PACK, M_OUT], F32, f"result{b}", f"raw{b}0") for b in range(BLOCKS)]
        gpsimd_tiles = [(0, 0), (0, 1), (0, 2)]
        y_sb = new_tile([P, len(gpsimd_tiles), M_OUT], F32, "y_sb", "raw20_0")
        first_term = placed_tile([P, M_OUT], F32, "first_term", 18)
        terms = placed_tile([P, 2, M_OUT], F32, "terms", 27)

        def finish_gpsimd(b, t):
            n = gpsimd_tiles.index((b, t))
            term = terms[:, n - 1, :] if n else first_term[:]
            if n < 1:
                nc.gpsimd.tensor_scalar(term, dest[b, t], skip_sb[:, b, t : t + 1], 0.0, MULT, ADD)
            else:
                nc.scalar.activation(term, dest[b, t], COPY, scale=skip_sb[:, b, t : t + 1])
            nc.scalar.copy(y_sb[:, n, :], y_banks[b * PACK + t][:])
            nc.gpsimd.tensor_tensor(result[b][:, t, :], term, y_sb[:, n, :], ADD)

        def finish_vector(b, t, parts):
            for n in range(parts):
                cols = slice(n * M_OUT // parts, (n + 1) * M_OUT // parts)
                nc.vector.scalar_tensor_tensor(
                    result[b][:, t, cols],
                    dest[b, t][:, cols],
                    skip_sb[:, b, t : t + 1],
                    y_banks[b * PACK + t][:, cols],
                    MULT,
                    ADD,
                )
                nc.sync.dma_start(out_rows[b, t][:, cols], result[b][:, t, cols])

        for b, t in gpsimd_tiles:
            finish_gpsimd(b, t)
        for b, t in gpsimd_tiles:
            nc.scalar.dma_start(out_rows[b, t], result[b][:, t, :])
        finish_vector(0, 3, 1)
        finish_vector(1, 0, 1)
        finish_vector(1, 1, 1)
        pick_dest(1, 3, dest[1, 0])
        finish_vector(1, 2, 1)
        finish_vector(1, 3, 2)
